import numpy as np
import ml_dtypes


def mxq(x, axis, fmt="e4m3"):
    dtype, down = {"e4m3": (ml_dtypes.float8_e4m3fn, 7), "e5m2": (ml_dtypes.float8_e5m2, 14)}[fmt]
    v = np.moveaxis(np.asarray(x, np.float32).astype(ml_dtypes.bfloat16).astype(np.float64), axis, -1)
    blocks = v.reshape(v.shape[:-1] + (-1, 32))
    amax = np.abs(blocks).max(-1, keepdims=True)
    byte = np.maximum(np.where(amax > 0, np.frexp(amax)[1] - 1 + 127, 0) - down, 1)
    scale = np.exp2(byte - 127.0)
    codes = (blocks / scale).astype(np.float32).astype(dtype).astype(np.float64)
    return np.moveaxis((codes * scale).reshape(v.shape), -1, axis)


WIDE = False


def mx_kscale(k):
    if not WIDE:
        return np.ones(k)
    levels = np.array([10, -10, 5, -5, 0])
    if k % 512:
        return np.exp2(np.random.permutation(np.resize(levels, k // 32))).repeat(32)
    a = np.empty((k // 512, 16))
    for p in range(k // 512):
        a[p, :8] = np.random.permutation(np.resize(levels, 8))
        for g in range(8):
            far = levels[np.abs(levels - a[p, g]) >= 10]
            a[p, g + 8] = far[np.random.randint(len(far))]
    return np.exp2(a.ravel()).repeat(32)


def f64(x):
    return np.asarray(x).astype(np.float64)


def striped(idx):
    return np.tile(np.asarray(idx).reshape(-1, 16).T, (8, 1)).astype(np.uint16)


def unstriped(offs):
    return offs[:16].T.reshape(-1).astype(np.int64)


E2M1 = np.array([0.0, 0.5, 1.0, 1.5, 2.0, 3.0, 4.0, 6.0, -0.0, -0.5, -1.0, -1.5, -2.0, -3.0, -4.0, -6.0])


def pack_weight(w, fmt):
    k, n = w.shape
    w = f64(np.asarray(w, np.float32).astype(ml_dtypes.bfloat16)).reshape(k // 32, 32, n)
    amax = np.abs(w).max(1)
    if fmt == "e4m3":
        byte = np.frexp(amax)[1] - 1 + 127 - 7
    else:
        mant, ex = np.frexp(amax / 6.0)
        byte = np.where(mant > 0.5, ex, ex - 1) + 127
    byte = np.clip(np.where(amax > 0, byte, 1), 1, 254)
    scaled = (w * np.exp2(127.0 - byte)[:, None, :]).reshape(k, n).astype(np.float32)
    by_word = np.ascontiguousarray(scaled.reshape(k // 512, 128, 4, n).transpose(0, 1, 3, 2))
    if fmt == "e4m3":
        words = by_word.astype(ml_dtypes.float8_e4m3fn).view(np.uint8)
    else:
        c = by_word.astype(ml_dtypes.float4_e2m1fn).view(np.uint8) & 0xF
        words = (c[..., 0::2] | (c[..., 1::2] << 4)).reshape(k // 512, 128, 2 * n)
    return np.ascontiguousarray(words), np.ascontiguousarray(byte.astype(np.uint8).reshape(k // 512, 16, n))


def unpack_weight(words, scales, fmt):
    g, _, n = scales.shape
    words = np.ascontiguousarray(words).reshape(g, 128, n, -1)
    if fmt == "e4m3":
        vals = words.view(ml_dtypes.float8_e4m3fn).astype(np.float64)
    else:
        nib = np.empty((g, 128, n, 4), np.uint8)
        nib[..., 0::2] = words & 0xF
        nib[..., 1::2] = words >> 4
        vals = E2M1[nib]
    vals = vals * np.repeat(np.exp2(scales.astype(np.float64) - 127.0), 8, axis=1)[..., None]
    return vals.transpose(0, 1, 3, 2).reshape(g * 512, n)


B, N, T, D, NQ = 2, 512, 2048, 512, 128


def setup_inputs():
    n = np.random.standard_normal
    jdx = np.random.permutation(1024)[:B * NQ]
    idx = np.random.permutation(T)[:B * N]
    s = mx_kscale(D)[:, None]
    kp = pack_weight(n((D, T)) / s, "e4m3")
    return {
        "qT": (n((D, 1024)) * s * (1.00 / np.sqrt(D))).astype(np.float32),
        "k_words": kp[0],
        "k_scales": kp[1],
        "kn": np.tile(np.random.uniform(1.0, 4.0, 2048), (128, 1)).astype(np.float32),
        "qn": (np.random.uniform(1.0, 4.0, (B, NQ, 1))).astype(np.float32),
        "offq": striped(jdx),
        "offs": striped(idx),
    }


def reference(qT, k_words, k_scales, kn, qn, offq, offs):
    jdx = unstriped(offq)
    idx = unstriped(offs)
    pick = lambda x, which: x[:, which].reshape(x.shape[0], B, -1).transpose(1, 0, 2)
    qg = mxq(pick(f64(qT), jdx), 1, "e4m3")
    k = unpack_weight(k_words, k_scales, "e4m3")
    kg = pick(k, idx)
    qq = qg
    a = qq.transpose(0, 2, 1) @ kg
    y = f64(qn) + pick(f64(kn), idx)[:, :1, :] - 2.0 * a
    return y

@@ -1,0 +1,133 @@
+from contextlib import ExitStack
+
+import concourse.mybir as mybir
+from concourse.masks import make_identity
+
+B, N, T, D, NQ, POOL = 2, 512, 2048, 512, 128, 1024
+FLOPS = 2 * B * NQ * N * D
+BYTES = D * POOL * 4 + D * T + (D // 32) * T + T * 4 + B * NQ * 4 + 128 * (16 + 64) * 2 + B * NQ * N * 4
+
+F32 = mybir.dt.float32
+BF16 = mybir.dt.bfloat16
+I32 = mybir.dt.int32
+U32 = mybir.dt.uint32
+U16 = mybir.dt.uint16
+U8 = mybir.dt.uint8
+FP8X4 = mybir.dt.float8_e4m3fn_x4
+COPY = mybir.ActivationFunctionType.Copy
+IDENTITY = mybir.ActivationFunctionType.Identity
+MULT = mybir.AluOpType.mult
+ADD = mybir.AluOpType.add
+
+P = 128
+KN_ROW = P - 1
+Q_CHUNKS = 2
+PIECES = ((0, 0, 512), (1, 0, 256), (1, 256, 256))
+
+
+def tile_attend_lq_dist_topk_kernel(tc, qT, k_words, k_scales, kn, qn, offq, offs, out):
+    nc = tc.nc
+    with ExitStack() as ctx:
+        sb = ctx.enter_context(tc.tile_pool(name="sb", bufs=1))
+        ps = ctx.enter_context(tc.psum_pool(name="ps", bufs=1))
+
+        offs_sb = sb.tile([P, B * N // 16], U16, name="offs_sb")
+        offq_sb = sb.tile([P, B * NQ // 16], U16, name="offq_sb")
+        kn_sb = sb.tile([P, T], F32, name="kn_sb")
+        ks_sb = sb.tile([P, T], U8, name="ks_sb", align_bytes=64)
+        kw_sb = sb.tile([P, T], I32, name="kw_sb", align_bytes=64)
+        qn_sb = sb.tile([P, B], F32, name="qn_sb")
+        ident = sb.tile([P, P], F32, name="ident")
+
+        nc.gpsimd.memset(ks_sb[:].bitcast(I32), 0)
+        nc.vector.memset(kn_sb[0:KN_ROW, :], 0.0)
+        make_identity(nc, ident[:])
+
+        nc.sync.dma_start(offs_sb[:], offs)
+        nc.sync.dma_start(kn_sb[KN_ROW:P, :], kn[0:1, :])
+        with nc.allow_non_contiguous_dma(reason="one value a partition"):
+            nc.gpsimd.dma_start(qn_sb[:], qn.rearrange("b q o -> q (b o)"))
+
+        q_rows = qT.rearrange("(p t) c -> p t c", t=4)
+        width = POOL // Q_CHUNKS
+        raws = []
+        for u in range(2):
+            if u == 1:
+                for r in range(4):
+                    nc.sync.dma_start(ks_sb[r:P:32, :].bitcast(I32), k_scales[0, r:16:4, :].bitcast(I32))
+                nc.sync.dma_start(offq_sb[:], offq)
+            for h in range(Q_CHUNKS):
+                raw = sb.tile([P, 2, width], F32, name=f"raw{u}{h}")
+                nc.sync.dma_start(raw[:], q_rows[:, 2 * u : 2 * u + 2, h * width : (h + 1) * width])
+                raws.append(raw)
+        nc.sync.dma_start(kw_sb[:], k_words[0].rearrange("p n t -> p (n t)").bitcast(I32))
+
+        pairs = [sb.tile([P, POOL, 2], BF16, name=f"pairs{u}") for u in range(2)]
+        for u in range(2):
+            for h in range(Q_CHUNKS):
+                nc.scalar.activation(
+                    pairs[u][:, h * width : (h + 1) * width, :],
+                    raws[u * Q_CHUNKS + h][:].rearrange("p e c -> p c e"),
+                    COPY,
+                )
+
+        kn_g = sb.tile([P, B * N], F32, name="kn_g")
+        nc.vector.tensor_copy(kn_g[:], kn_sb[:].indirect(offs_sb[:]))
+        ks_g = sb.tile([P, B * N], U8, name="ks_g", align_bytes=64)
+        nc.vector.tensor_copy(ks_g[:], ks_sb[:].indirect(offs_sb[:]))
+
+        norms = []
+        for b in range(B):
+            turned = ps.tile([P, 4, P], F32, name=f"turned{b}")
+            for j in range(4):
+                nc.tensor.transpose(turned[:, j, :], kn_g[:, b * N + j * P : b * N + (j + 1) * P], ident[:])
+            kn_col = sb.tile([P, 4], F32, name=f"kn_col{b}")
+            nc.scalar.activation(kn_col[:], turned[:, :, KN_ROW], COPY)
+            spread = ps.tile([P, N], F32, name=f"spread{b}")
+            for j in range(4):
+                nc.tensor.transpose(spread[:, j * P : (j + 1) * P], kn_col[:, j : j + 1].to_broadcast([P, P]), ident[:])
+            norm = sb.tile([P, N], F32, name=f"norm{b}")
+            nc.scalar.activation(norm[:], spread[:], IDENTITY, bias=qn_sb[:, b : b + 1])
+            norms.append(norm)
+
+        q_g = sb.tile([P, B * NQ, 4], BF16, name="q_g", align_bytes=64)
+        q_g_words = q_g[:].rearrange("p n t -> p (n t)").bitcast(U32).rearrange("p (n u) -> p n u", u=2)
+        for u in range(2):
+            window = pairs[u][:].rearrange("p c e -> p (c e)").bitcast(U32)
+            nc.vector.tensor_copy(q_g_words[:, :, u], window.indirect(offq_sb[:]))
+        q_codes = sb.tile([P, B * NQ], U32, name="q_codes", align_bytes=64)
+        q_scales = sb.tile([P, B * NQ], U8, name="q_scales", align_bytes=64)
+        nc.vector.quantize_mx(
+            out=q_codes[:].bitcast(FP8X4),
+            scales=q_scales[:],
+            in_=q_g[:].rearrange("p n t -> p (n t)"),
+        )
+
+        def product(i):
+            b, n0, n = PIECES[i]
+            s0 = b * N + n0
+            kw_g = sb.tile([P, n], U32, name=f"kw_g{i}", align_bytes=64)
+            nc.vector.tensor_copy(kw_g[:], kw_sb[:].bitcast(U32).indirect(offs_sb[:, s0 // 16 : (s0 + n) // 16]))
+            acc = ps.tile([P, n], F32, name=f"acc{i}")
+            nc.tensor.matmul_mx(
+                out=acc[:],
+                lhsT=q_codes[:, b * NQ : (b + 1) * NQ].bitcast(FP8X4),
+                lhsT_scale=q_scales[:, b * NQ : (b + 1) * NQ],
+                rhs=kw_g[:].bitcast(FP8X4),
+                rhs_scale=ks_g[:, s0 : s0 + n],
+                start=True,
+                stop=True,
+            )
+            return acc
+
+        def finish(i, acc):
+            b, n0, n = PIECES[i]
+            res = sb.tile([P, n], F32, name=f"res{i}")
+            nc.vector.scalar_tensor_tensor(res[:], acc[:], -2.0, norms[b][:, n0 : n0 + n], MULT, ADD)
+            nc.sync.dma_start(out[b, :, n0 : n0 + n], res[:])
+
+        accs = [product(0)]
+        for i in range(1, len(PIECES)):
+            accs.append(product(i))
+            finish(i - 1, accs[i - 1])
+        finish(len(PIECES) - 1, accs[-1])

@@ -36,17 +36,17 @@ def tile_attend_lq_dist_topk_kernel(tc, qT, k_words, k_scales, kn, qn, offq, off
         kn_sb = sb.tile([P, T], F32, name="kn_sb")
         ks_sb = sb.tile([P, T], U8, name="ks_sb", align_bytes=64)
         kw_sb = sb.tile([P, T], I32, name="kw_sb", align_bytes=64)
-        qn_sb = sb.tile([P, B], F32, name="qn_sb")
+        qn_row = sb.tile([P, B * NQ], F32, name="qn_row")
         ident = sb.tile([P, P], F32, name="ident")
 
-        nc.gpsimd.memset(ks_sb[:].bitcast(I32), 0)
+        nc.vector.memset(ks_sb[:].bitcast(I32), 0)
         nc.vector.memset(kn_sb[0:KN_ROW, :], 0.0)
         make_identity(nc, ident[:])
+        nc.gpsimd.memset(qn_row[0:KN_ROW, :], 0.0)
 
         nc.sync.dma_start(offs_sb[:], offs)
         nc.sync.dma_start(kn_sb[KN_ROW:P, :], kn[0:1, :])
-        with nc.allow_non_contiguous_dma(reason="one value a partition"):
-            nc.gpsimd.dma_start(qn_sb[:], qn.rearrange("b q o -> q (b o)"))
+        nc.scalar.dma_start(qn_row[KN_ROW:P, :], qn.rearrange("b q o -> o (b q)"))
 
         q_rows = qT.rearrange("(p t) c -> p t c", t=4)
         width = POOL // Q_CHUNKS
@@ -57,7 +57,7 @@ def tile_attend_lq_dist_topk_kernel(tc, qT, k_words, k_scales, kn, qn, offq, off
                     nc.sync.dma_start(ks_sb[r:P:32, :].bitcast(I32), k_scales[0, r:16:4, :].bitcast(I32))
                 nc.sync.dma_start(offq_sb[:], offq)
             for h in range(Q_CHUNKS):
-                raw = sb.tile([P, 2, width], F32, name=f"raw{u}{h}")
+                raw = sb.tile([P, 2, width], F32, name=f"raw{u}{h}", tag="last_raw" if (u, h) == (1, Q_CHUNKS - 1) else f"raw{u}{h}")
                 nc.sync.dma_start(raw[:], q_rows[:, 2 * u : 2 * u + 2, h * width : (h + 1) * width])
                 raws.append(raw)
         nc.sync.dma_start(kw_sb[:], k_words[0].rearrange("p n t -> p (n t)").bitcast(I32))
@@ -76,20 +76,6 @@ def tile_attend_lq_dist_topk_kernel(tc, qT, k_words, k_scales, kn, qn, offq, off
         ks_g = sb.tile([P, B * N], U8, name="ks_g", align_bytes=64)
         nc.vector.tensor_copy(ks_g[:], ks_sb[:].indirect(offs_sb[:]))
 
-        norms = []
-        for b in range(B):
-            turned = ps.tile([P, 4, P], F32, name=f"turned{b}")
-            for j in range(4):
-                nc.tensor.transpose(turned[:, j, :], kn_g[:, b * N + j * P : b * N + (j + 1) * P], ident[:])
-            kn_col = sb.tile([P, 4], F32, name=f"kn_col{b}")
-            nc.scalar.activation(kn_col[:], turned[:, :, KN_ROW], COPY)
-            spread = ps.tile([P, N], F32, name=f"spread{b}")
-            for j in range(4):
-                nc.tensor.transpose(spread[:, j * P : (j + 1) * P], kn_col[:, j : j + 1].to_broadcast([P, P]), ident[:])
-            norm = sb.tile([P, N], F32, name=f"norm{b}")
-            nc.scalar.activation(norm[:], spread[:], IDENTITY, bias=qn_sb[:, b : b + 1])
-            norms.append(norm)
-
         q_g = sb.tile([P, B * NQ, 4], BF16, name="q_g", align_bytes=64)
         q_g_words = q_g[:].rearrange("p n t -> p (n t)").bitcast(U32).rearrange("p (n u) -> p n u", u=2)
         for u in range(2):
@@ -102,6 +88,27 @@ def tile_attend_lq_dist_topk_kernel(tc, qT, k_words, k_scales, kn, qn, offq, off
             scales=q_scales[:],
             in_=q_g[:].rearrange("p n t -> p (n t)"),
         )
+
+        turned = [ps.tile([P, 4, P], F32, name=f"turned{b}") for b in range(B)]
+        qn_turned = ps.tile([P, B, P], F32, name="qn_turned")
+        for b in range(B):
+            nc.tensor.transpose(qn_turned[:, b, :], qn_row[:, b * NQ : (b + 1) * NQ], ident[:])
+        for b in range(B):
+            for j in range(4):
+                nc.tensor.transpose(turned[b][:, j, :], kn_g[:, b * N + j * P : b * N + (j + 1) * P], ident[:])
+        cols = sb.tile([P, 4 * B + B], F32, name="cols", tag="last_raw")
+        for b in range(B):
+            nc.scalar.activation(cols[:, 4 * b : 4 * b + 4], turned[b][:, :, KN_ROW], COPY)
+        nc.scalar.activation(cols[:, 4 * B : 4 * B + B], qn_turned[:, :, KN_ROW], COPY)
+        norms = []
+        for b in range(B):
+            spread = ps.tile([P, N], F32, name=f"spread{b}")
+            for j in range(4):
+                column = cols[:, 4 * b + j : 4 * b + j + 1]
+                nc.tensor.transpose(spread[:, j * P : (j + 1) * P], column.to_broadcast([P, P]), ident[:])
+            norm = sb.tile([P, N], F32, name=f"norm{b}")
+            nc.scalar.activation(norm[:], spread[:], IDENTITY, bias=cols[:, 4 * B + b : 4 * B + b + 1])
+            norms.append(norm)
 
         def product(i):
             b, n0, n = PIECES[i]
@@ -126,8 +133,6 @@ def tile_attend_lq_dist_topk_kernel(tc, qT, k_words, k_scales, kn, qn, offq, off
             nc.vector.scalar_tensor_tensor(res[:], acc[:], -2.0, norms[b][:, n0 : n0 + n], MULT, ADD)
             nc.sync.dma_start(out[b, :, n0 : n0 + n], res[:])
 
-        accs = [product(0)]
-        for i in range(1, len(PIECES)):
-            accs.append(product(i))
-            finish(i - 1, accs[i - 1])
-        finish(len(PIECES) - 1, accs[-1])
+        accs = [product(i) for i in range(len(PIECES))]
+        for i in range(len(PIECES)):
+            finish(i, accs[i])

@@ -21,8 +21,8 @@ ADD = mybir.AluOpType.add
 
 P = 128
 KN_ROW = P - 1
-Q_CHUNKS = 2
-PIECES = ((0, 0, 512), (1, 0, 256), (1, 256, 256))
+LATE_CHUNKS = ((0, 256), (256, 256), (512, 256), (768, 256))
+PIECE = 256
 
 
 def tile_attend_lq_dist_topk_kernel(tc, qT, k_words, k_scales, kn, qn, offq, offs, out):
@@ -44,95 +44,88 @@ def tile_attend_lq_dist_topk_kernel(tc, qT, k_words, k_scales, kn, qn, offq, off
         make_identity(nc, ident[:])
         nc.gpsimd.memset(qn_row[0:KN_ROW, :], 0.0)
 
+        q_rows = qT.rearrange("(p t) c -> p t c", t=4)
         nc.sync.dma_start(offs_sb[:], offs)
         nc.sync.dma_start(kn_sb[KN_ROW:P, :], kn[0:1, :])
         nc.scalar.dma_start(qn_row[KN_ROW:P, :], qn.rearrange("b q o -> o (b q)"))
-
-        q_rows = qT.rearrange("(p t) c -> p t c", t=4)
-        width = POOL // Q_CHUNKS
-        raws = []
-        for u in range(2):
-            if u == 1:
-                for r in range(4):
-                    nc.sync.dma_start(ks_sb[r:P:32, :].bitcast(I32), k_scales[0, r:16:4, :].bitcast(I32))
-                nc.sync.dma_start(offq_sb[:], offq)
-            for h in range(Q_CHUNKS):
-                raw = sb.tile([P, 2, width], F32, name=f"raw{u}{h}", tag="last_raw" if (u, h) == (1, Q_CHUNKS - 1) else f"raw{u}{h}")
-                nc.sync.dma_start(raw[:], q_rows[:, 2 * u : 2 * u + 2, h * width : (h + 1) * width])
-                raws.append(raw)
+        early = []
+        for t in range(2):
+            raw = sb.tile([P, POOL], F32, name=f"early{t}")
+            nc.sync.dma_start(raw[:], q_rows[:, t, :])
+            early.append(raw)
+        for r in range(4):
+            nc.sync.dma_start(ks_sb[r:P:32, :].bitcast(I32), k_scales[0, r:16:4, :].bitcast(I32))
+        nc.sync.dma_start(offq_sb[:], offq)
         nc.sync.dma_start(kw_sb[:], k_words[0].rearrange("p n t -> p (n t)").bitcast(I32))
+        late = []
+        for h, (c0, width) in enumerate(LATE_CHUNKS):
+            raw = sb.tile([P, 2, width], F32, name=f"late{h}")
+            nc.sync.dma_start(raw[:], q_rows[:, 2:4, c0 : c0 + width])
+            late.append(raw)
 
-        pairs = [sb.tile([P, POOL, 2], BF16, name=f"pairs{u}") for u in range(2)]
-        for u in range(2):
-            for h in range(Q_CHUNKS):
-                nc.scalar.activation(
-                    pairs[u][:, h * width : (h + 1) * width, :],
-                    raws[u * Q_CHUNKS + h][:].rearrange("p e c -> p c e"),
-                    COPY,
-                )
+        planes = [sb.tile([P, POOL], BF16, name=f"plane{t}") for t in range(2)]
+        for t in range(2):
+            nc.scalar.activation(planes[t][:], early[t][:], COPY)
+        q_g = [sb.tile([P, NQ, 4], BF16, name=f"q_g{b}", align_bytes=64) for b in range(B)]
+        for t in range(2):
+            for b in range(B):
+                nc.scalar.activation(q_g[b][:, :, t], planes[t][:].indirect(offq_sb[:, b * 8 : b * 8 + 8]), COPY)
 
         kn_g = sb.tile([P, B * N], F32, name="kn_g")
         nc.vector.tensor_copy(kn_g[:], kn_sb[:].indirect(offs_sb[:]))
         ks_g = sb.tile([P, B * N], U8, name="ks_g", align_bytes=64)
         nc.vector.tensor_copy(ks_g[:], ks_sb[:].indirect(offs_sb[:]))
+        kw_g = sb.tile([P, B * N], U32, name="kw_g", align_bytes=64)
+        nc.vector.tensor_copy(kw_g[:], kw_sb[:].bitcast(U32).indirect(offs_sb[:]))
 
-        q_g = sb.tile([P, B * NQ, 4], BF16, name="q_g", align_bytes=64)
-        q_g_words = q_g[:].rearrange("p n t -> p (n t)").bitcast(U32).rearrange("p (n u) -> p n u", u=2)
-        for u in range(2):
-            window = pairs[u][:].rearrange("p c e -> p (c e)").bitcast(U32)
-            nc.vector.tensor_copy(q_g_words[:, :, u], window.indirect(offq_sb[:]))
-        q_codes = sb.tile([P, B * NQ], U32, name="q_codes", align_bytes=64)
-        q_scales = sb.tile([P, B * NQ], U8, name="q_scales", align_bytes=64)
-        nc.vector.quantize_mx(
-            out=q_codes[:].bitcast(FP8X4),
-            scales=q_scales[:],
-            in_=q_g[:].rearrange("p n t -> p (n t)"),
-        )
-
-        turned = [ps.tile([P, 4, P], F32, name=f"turned{b}") for b in range(B)]
-        qn_turned = ps.tile([P, B, P], F32, name="qn_turned")
+        turned = [ps.tile([P, 4, P], F32, name=f"turned{b}", tag=f"bank{b}") for b in range(B)]
+        qn_turned = ps.tile([P, B, P], F32, name="qn_turned", tag="bank2")
         for b in range(B):
             nc.tensor.transpose(qn_turned[:, b, :], qn_row[:, b * NQ : (b + 1) * NQ], ident[:])
         for b in range(B):
             for j in range(4):
                 nc.tensor.transpose(turned[b][:, j, :], kn_g[:, b * N + j * P : b * N + (j + 1) * P], ident[:])
-        cols = sb.tile([P, 4 * B + B], F32, name="cols", tag="last_raw")
+        cols = sb.tile([P, 4 * B + B], F32, name="cols", tag="plane1")
         for b in range(B):
             nc.scalar.activation(cols[:, 4 * b : 4 * b + 4], turned[b][:, :, KN_ROW], COPY)
         nc.scalar.activation(cols[:, 4 * B : 4 * B + B], qn_turned[:, :, KN_ROW], COPY)
-        norms = []
+        spreads = [ps.tile([P, N], F32, name=f"spread{b}") for b in range(B)]
         for b in range(B):
-            spread = ps.tile([P, N], F32, name=f"spread{b}")
             for j in range(4):
                 column = cols[:, 4 * b + j : 4 * b + j + 1]
-                nc.tensor.transpose(spread[:, j * P : (j + 1) * P], column.to_broadcast([P, P]), ident[:])
-            norm = sb.tile([P, N], F32, name=f"norm{b}")
-            nc.scalar.activation(norm[:], spread[:], IDENTITY, bias=cols[:, 4 * B + b : 4 * B + b + 1])
-            norms.append(norm)
+                nc.tensor.transpose(spreads[b][:, j * P : (j + 1) * P], column.to_broadcast([P, P]), ident[:])
 
-        def product(i):
-            b, n0, n = PIECES[i]
-            s0 = b * N + n0
-            kw_g = sb.tile([P, n], U32, name=f"kw_g{i}", align_bytes=64)
-            nc.vector.tensor_copy(kw_g[:], kw_sb[:].bitcast(U32).indirect(offs_sb[:, s0 // 16 : (s0 + n) // 16]))
-            acc = ps.tile([P, n], F32, name=f"acc{i}")
+        pairs = sb.tile([P, POOL, 2], BF16, name="pairs")
+        for h, (c0, width) in enumerate(LATE_CHUNKS):
+            nc.scalar.activation(pairs[:, c0 : c0 + width, :], late[h][:].rearrange("p e c -> p c e"), COPY)
+        norms = sb.tile([P, B, N], F32, name="norms", tag=f"late{len(LATE_CHUNKS) - 1}")
+        for b in range(B):
+            nc.scalar.activation(norms[:, b, :], spreads[b][:], IDENTITY, bias=cols[:, 4 * B + b : 4 * B + b + 1])
+        window = pairs[:].rearrange("p c e -> p (c e)").bitcast(U32)
+        for b in range(B):
+            words = q_g[b][:].rearrange("p n t -> p (n t)").bitcast(U32).rearrange("p (n u) -> p n u", u=2)
+            nc.vector.tensor_copy(words[:, :, 1], window.indirect(offq_sb[:, b * 8 : b * 8 + 8]))
+        q_codes, q_scales = [], []
+        for b in range(B):
+            codes = sb.tile([P, NQ], U32, name=f"q_codes{b}", align_bytes=64)
+            scales = sb.tile([P, NQ], U8, name=f"q_scales{b}", align_bytes=64)
+            nc.vector.quantize_mx(out=codes[:].bitcast(FP8X4), scales=scales[:], in_=q_g[b][:].rearrange("p n t -> p (n t)"))
+            q_codes.append(codes)
+            q_scales.append(scales)
+
+        for i in range(B * N // PIECE):
+            s0 = i * PIECE
+            b, n0 = divmod(s0, N)
+            acc = ps.tile([P, PIECE], F32, name=f"acc{i}", tag=f"bank{i}")
             nc.tensor.matmul_mx(
                 out=acc[:],
-                lhsT=q_codes[:, b * NQ : (b + 1) * NQ].bitcast(FP8X4),
-                lhsT_scale=q_scales[:, b * NQ : (b + 1) * NQ],
-                rhs=kw_g[:].bitcast(FP8X4),
-                rhs_scale=ks_g[:, s0 : s0 + n],
+                lhsT=q_codes[b][:].bitcast(FP8X4),
+                lhsT_scale=q_scales[b][:],
+                rhs=kw_g[:, s0 : s0 + PIECE].bitcast(FP8X4),
+                rhs_scale=ks_g[:, s0 : s0 + PIECE],
                 start=True,
                 stop=True,
             )
-            return acc
-
-        def finish(i, acc):
-            b, n0, n = PIECES[i]
-            res = sb.tile([P, n], F32, name=f"res{i}")
-            nc.vector.scalar_tensor_tensor(res[:], acc[:], -2.0, norms[b][:, n0 : n0 + n], MULT, ADD)
-            nc.sync.dma_start(out[b, :, n0 : n0 + n], res[:])
-
-        accs = [product(i) for i in range(len(PIECES))]
-        for i in range(len(PIECES)):
-            finish(i, accs[i])
+            res = sb.tile([P, PIECE], F32, name=f"res{i}")
+            nc.vector.scalar_tensor_tensor(res[:], acc[:], -2.0, norms[:, b, n0 : n0 + PIECE], MULT, ADD)
+            nc.sync.dma_start(out[b, :, n0 : n0 + PIECE], res[:])

@@ -21,7 +21,6 @@ ADD = mybir.AluOpType.add
 
 P = 128
 KN_ROW = P - 1
-LATE_CHUNKS = ((0, 256), (256, 256), (512, 256), (768, 256))
 PIECE = 256
 
 
@@ -58,9 +57,9 @@ def tile_attend_lq_dist_topk_kernel(tc, qT, k_words, k_scales, kn, qn, offq, off
         nc.sync.dma_start(offq_sb[:], offq)
         nc.sync.dma_start(kw_sb[:], k_words[0].rearrange("p n t -> p (n t)").bitcast(I32))
         late = []
-        for h, (c0, width) in enumerate(LATE_CHUNKS):
-            raw = sb.tile([P, 2, width], F32, name=f"late{h}")
-            nc.sync.dma_start(raw[:], q_rows[:, 2:4, c0 : c0 + width])
+        for t in (2, 3):
+            raw = sb.tile([P, POOL], F32, name=f"late{t}")
+            nc.sync.dma_start(raw[:], q_rows[:, t, :])
             late.append(raw)
 
         planes = [sb.tile([P, POOL], BF16, name=f"plane{t}") for t in range(2)]
@@ -95,16 +94,13 @@ def tile_attend_lq_dist_topk_kernel(tc, qT, k_words, k_scales, kn, qn, offq, off
                 column = cols[:, 4 * b + j : 4 * b + j + 1]
                 nc.tensor.transpose(spreads[b][:, j * P : (j + 1) * P], column.to_broadcast([P, P]), ident[:])
 
-        pairs = sb.tile([P, POOL, 2], BF16, name="pairs")
-        for h, (c0, width) in enumerate(LATE_CHUNKS):
-            nc.scalar.activation(pairs[:, c0 : c0 + width, :], late[h][:].rearrange("p e c -> p c e"), COPY)
-        norms = sb.tile([P, B, N], F32, name="norms", tag=f"late{len(LATE_CHUNKS) - 1}")
+        norms = sb.tile([P, B, N], F32, name="norms")
         for b in range(B):
             nc.scalar.activation(norms[:, b, :], spreads[b][:], IDENTITY, bias=cols[:, 4 * B + b : 4 * B + b + 1])
-        window = pairs[:].rearrange("p c e -> p (c e)").bitcast(U32)
-        for b in range(B):
-            words = q_g[b][:].rearrange("p n t -> p (n t)").bitcast(U32).rearrange("p (n u) -> p n u", u=2)
-            nc.vector.tensor_copy(words[:, :, 1], window.indirect(offq_sb[:, b * 8 : b * 8 + 8]))
+
+        for t in (2, 3):
+            for b in range(B):
+                nc.vector.tensor_copy(q_g[b][:, :, t], late[t - 2][:].indirect(offq_sb[:, b * 8 : b * 8 + 8]))
         q_codes, q_scales = [], []
         for b in range(B):
             codes = sb.tile([P, NQ], U32, name=f"q_codes{b}", align_bytes=64)

@@ -36,11 +36,13 @@ def tile_attend_lq_dist_topk_kernel(tc, qT, k_words, k_scales, kn, qn, offq, off
         ks_sb = sb.tile([P, T], U8, name="ks_sb", align_bytes=64)
         kw_sb = sb.tile([P, T], I32, name="kw_sb", align_bytes=64)
         qn_row = sb.tile([P, B * NQ], F32, name="qn_row")
+        ks_plane = sb.tile([P, B * N], U8, name="ks_plane", align_bytes=64)
         ident = sb.tile([P, P], F32, name="ident")
 
-        nc.vector.memset(ks_sb[:].bitcast(I32), 0)
+        nc.gpsimd.memset(ks_sb[:].bitcast(I32), 0)
         nc.vector.memset(kn_sb[0:KN_ROW, :], 0.0)
         make_identity(nc, ident[:])
+        nc.gpsimd.memset(ks_plane[:].bitcast(I32), 0)
         nc.gpsimd.memset(qn_row[0:KN_ROW, :], 0.0)
 
         q_rows = qT.rearrange("(p t) c -> p t c", t=4)
@@ -52,30 +54,31 @@ def tile_attend_lq_dist_topk_kernel(tc, qT, k_words, k_scales, kn, qn, offq, off
             raw = sb.tile([P, POOL], F32, name=f"early{t}")
             nc.sync.dma_start(raw[:], q_rows[:, t, :])
             early.append(raw)
-        for r in range(4):
-            nc.sync.dma_start(ks_sb[r:P:32, :].bitcast(I32), k_scales[0, r:16:4, :].bitcast(I32))
+        nc.sync.dma_start(ks_sb[0:P:8, :].bitcast(I32), k_scales[0].bitcast(I32))
         nc.sync.dma_start(offq_sb[:], offq)
         nc.sync.dma_start(kw_sb[:], k_words[0].rearrange("p n t -> p (n t)").bitcast(I32))
         late = []
         for t in (2, 3):
-            raw = sb.tile([P, POOL], F32, name=f"late{t}")
+            raw = sb.tile([P, POOL], F32, name=f"late{t}", align_bytes=64)
             nc.sync.dma_start(raw[:], q_rows[:, t, :])
             late.append(raw)
 
         planes = [sb.tile([P, POOL], BF16, name=f"plane{t}") for t in range(2)]
         for t in range(2):
             nc.scalar.activation(planes[t][:], early[t][:], COPY)
-        q_g = [sb.tile([P, NQ, 4], BF16, name=f"q_g{b}", align_bytes=64) for b in range(B)]
+        q_g = sb.tile([P, B * NQ, 4], BF16, name="q_g", align_bytes=64)
         for t in range(2):
-            for b in range(B):
-                nc.scalar.activation(q_g[b][:, :, t], planes[t][:].indirect(offq_sb[:, b * 8 : b * 8 + 8]), COPY)
+            nc.scalar.activation(q_g[:, :, t], planes[t][:].indirect(offq_sb[:]), COPY)
 
         kn_g = sb.tile([P, B * N], F32, name="kn_g")
         nc.vector.tensor_copy(kn_g[:], kn_sb[:].indirect(offs_sb[:]))
         ks_g = sb.tile([P, B * N], U8, name="ks_g", align_bytes=64)
         nc.vector.tensor_copy(ks_g[:], ks_sb[:].indirect(offs_sb[:]))
-        kw_g = sb.tile([P, B * N], U32, name="kw_g", align_bytes=64)
-        nc.vector.tensor_copy(kw_g[:], kw_sb[:].bitcast(U32).indirect(offs_sb[:]))
+        for r in range(4):
+            nc.sync.dma_start(ks_plane[r:P:32, :].bitcast(I32), ks_g[8 * r : P : 32, :].bitcast(I32))
+        held = B * N - PIECE
+        kw_g = sb.tile([P, held], U32, name="kw_g", align_bytes=64)
+        nc.vector.tensor_copy(kw_g[:], kw_sb[:].bitcast(U32).indirect(offs_sb[:, : held // 16]))
 
         turned = [ps.tile([P, 4, P], F32, name=f"turned{b}", tag=f"bank{b}") for b in range(B)]
         qn_turned = ps.tile([P, B, P], F32, name="qn_turned", tag="bank2")
@@ -98,16 +101,18 @@ def tile_attend_lq_dist_topk_kernel(tc, qT, k_words, k_scales, kn, qn, offq, off
         for b in range(B):
             nc.scalar.activation(norms[:, b, :], spreads[b][:], IDENTITY, bias=cols[:, 4 * B + b : 4 * B + b + 1])
 
-        for t in (2, 3):
-            for b in range(B):
-                nc.vector.tensor_copy(q_g[b][:, :, t], late[t - 2][:].indirect(offq_sb[:, b * 8 : b * 8 + 8]))
+        nc.vector.tensor_copy(q_g[:, :, 2], late[0][:].indirect(offq_sb[:]))
+        for b in range(B):
+            nc.vector.tensor_copy(q_g[:, b * NQ : (b + 1) * NQ, 3], late[1][:].indirect(offq_sb[:, b * 8 : b * 8 + 8]))
         q_codes, q_scales = [], []
         for b in range(B):
             codes = sb.tile([P, NQ], U32, name=f"q_codes{b}", align_bytes=64)
             scales = sb.tile([P, NQ], U8, name=f"q_scales{b}", align_bytes=64)
-            nc.vector.quantize_mx(out=codes[:].bitcast(FP8X4), scales=scales[:], in_=q_g[b][:].rearrange("p n t -> p (n t)"))
+            nc.vector.quantize_mx(out=codes[:].bitcast(FP8X4), scales=scales[:], in_=q_g[:, b * NQ : (b + 1) * NQ, :].rearrange("p n t -> p (n t)"))
             q_codes.append(codes)
             q_scales.append(scales)
+        kw_last = sb.tile([P, PIECE], U32, name="kw_last", tag="late3", align_bytes=64)
+        nc.vector.tensor_copy(kw_last[:], kw_sb[:].bitcast(U32).indirect(offs_sb[:, held // 16 :]))
 
         for i in range(B * N // PIECE):
             s0 = i * PIECE
@@ -117,8 +122,8 @@ def tile_attend_lq_dist_topk_kernel(tc, qT, k_words, k_scales, kn, qn, offq, off
                 out=acc[:],
                 lhsT=q_codes[b][:].bitcast(FP8X4),
                 lhsT_scale=q_scales[b][:],
-                rhs=kw_g[:, s0 : s0 + PIECE].bitcast(FP8X4),
-                rhs_scale=ks_g[:, s0 : s0 + PIECE],
+                rhs=(kw_g[:, s0 : s0 + PIECE] if s0 < held else kw_last[:]).bitcast(FP8X4),
+                rhs_scale=ks_plane[:, s0 : s0 + PIECE],
                 start=True,
                 stop=True,
             )

@@ -35,7 +35,7 @@ def tile_attend_lq_dist_topk_kernel(tc, qT, k_words, k_scales, kn, qn, offq, off
         kn_sb = sb.tile([P, T], F32, name="kn_sb")
         ks_sb = sb.tile([P, T], U8, name="ks_sb", align_bytes=64)
         kw_sb = sb.tile([P, T], I32, name="kw_sb", align_bytes=64)
-        qn_row = sb.tile([P, B * NQ], F32, name="qn_row")
+        qn_rows = sb.tile([P, NQ], F32, name="qn_rows")
         ks_plane = sb.tile([P, B * N], U8, name="ks_plane", align_bytes=64)
         ident = sb.tile([P, P], F32, name="ident")
 
@@ -43,12 +43,12 @@ def tile_attend_lq_dist_topk_kernel(tc, qT, k_words, k_scales, kn, qn, offq, off
         nc.vector.memset(kn_sb[0:KN_ROW, :], 0.0)
         make_identity(nc, ident[:])
         nc.gpsimd.memset(ks_plane[:].bitcast(I32), 0)
-        nc.gpsimd.memset(qn_row[0:KN_ROW, :], 0.0)
+        nc.gpsimd.memset(qn_rows[0 : P - B, :], 0.0)
 
         q_rows = qT.rearrange("(p t) c -> p t c", t=4)
         nc.sync.dma_start(offs_sb[:], offs)
-        nc.sync.dma_start(kn_sb[KN_ROW:P, :], kn[0:1, :])
-        nc.scalar.dma_start(qn_row[KN_ROW:P, :], qn.rearrange("b q o -> o (b q)"))
+        nc.scalar.dma_start(kn_sb[KN_ROW:P, :], kn[0:1, :])
+        nc.scalar.dma_start(qn_rows[P - B : P, :], qn.rearrange("b q o -> b (q o)"))
         early = []
         for t in range(2):
             raw = sb.tile([P, POOL], F32, name=f"early{t}")
@@ -81,23 +81,22 @@ def tile_attend_lq_dist_topk_kernel(tc, qT, k_words, k_scales, kn, qn, offq, off
         nc.vector.tensor_copy(kw_g[:], kw_sb[:].bitcast(U32).indirect(offs_sb[:, : held // 16]))
 
         turned = [ps.tile([P, 4, P], F32, name=f"turned{b}", tag=f"bank{b}") for b in range(B)]
-        qn_turned = ps.tile([P, B, P], F32, name="qn_turned", tag="bank2")
-        for b in range(B):
-            nc.tensor.transpose(qn_turned[:, b, :], qn_row[:, b * NQ : (b + 1) * NQ], ident[:])
+        qn_turned = ps.tile([P, P], F32, name="qn_turned", tag="bank2")
+        nc.tensor.transpose(qn_turned[:], qn_rows[:], ident[:])
         for b in range(B):
             for j in range(4):
                 nc.tensor.transpose(turned[b][:, j, :], kn_g[:, b * N + j * P : b * N + (j + 1) * P], ident[:])
-        cols = sb.tile([P, 4 * B + B], F32, name="cols", tag="plane1")
+        cols = sb.tile([P, 4 * B + B], F32, name="cols", tag="plane0")
         for b in range(B):
             nc.scalar.activation(cols[:, 4 * b : 4 * b + 4], turned[b][:, :, KN_ROW], COPY)
-        nc.scalar.activation(cols[:, 4 * B : 4 * B + B], qn_turned[:, :, KN_ROW], COPY)
+        nc.scalar.activation(cols[:, 4 * B : 4 * B + B], qn_turned[:, P - B : P], COPY)
         spreads = [ps.tile([P, N], F32, name=f"spread{b}") for b in range(B)]
         for b in range(B):
             for j in range(4):
                 column = cols[:, 4 * b + j : 4 * b + j + 1]
                 nc.tensor.transpose(spreads[b][:, j * P : (j + 1) * P], column.to_broadcast([P, P]), ident[:])
 
-        norms = sb.tile([P, B, N], F32, name="norms")
+        norms = sb.tile([P, B, N], F32, name="norms", tag="plane1")
         for b in range(B):
             nc.scalar.activation(norms[:, b, :], spreads[b][:], IDENTITY, bias=cols[:, 4 * B + b : 4 * B + b + 1])
 

@@ -20,7 +20,10 @@ MULT = mybir.AluOpType.mult
 ADD = mybir.AluOpType.add
 
 P = 128
+LIST_ROWS = 16
 KN_ROW = P - 1
+QN_ROW = P - B
+CHUNKS = N // P
 PIECE = 256
 
 
@@ -30,99 +33,107 @@ def tile_attend_lq_dist_topk_kernel(tc, qT, k_words, k_scales, kn, qn, offq, off
         sb = ctx.enter_context(tc.tile_pool(name="sb", bufs=1))
         ps = ctx.enter_context(tc.psum_pool(name="ps", bufs=1))
 
-        offs_sb = sb.tile([P, B * N // 16], U16, name="offs_sb")
-        offq_sb = sb.tile([P, B * NQ // 16], U16, name="offq_sb")
+        offs_sb = sb.tile([P, B * N // LIST_ROWS], U16, name="offs_sb")
+        offq_sb = sb.tile([P, B * NQ // LIST_ROWS], U16, name="offq_sb")
         kn_sb = sb.tile([P, T], F32, name="kn_sb")
         ks_sb = sb.tile([P, T], U8, name="ks_sb", align_bytes=64)
         kw_sb = sb.tile([P, T], I32, name="kw_sb", align_bytes=64)
         qn_rows = sb.tile([P, NQ], F32, name="qn_rows")
-        ks_plane = sb.tile([P, B * N], U8, name="ks_plane", align_bytes=64)
+        ks_operand = sb.tile([P, B * N], U8, name="ks_operand", align_bytes=64)
         ident = sb.tile([P, P], F32, name="ident")
 
         nc.gpsimd.memset(ks_sb[:].bitcast(I32), 0)
         nc.vector.memset(kn_sb[0:KN_ROW, :], 0.0)
         make_identity(nc, ident[:])
-        nc.gpsimd.memset(ks_plane[:].bitcast(I32), 0)
-        nc.gpsimd.memset(qn_rows[0 : P - B, :], 0.0)
+        nc.gpsimd.memset(ks_operand[:].bitcast(I32), 0)
+        nc.gpsimd.memset(qn_rows[0:QN_ROW, :], 0.0)
 
-        q_rows = qT.rearrange("(p t) c -> p t c", t=4)
+        q_planes = qT.rearrange("(p t) c -> p t c", t=4)
         nc.sync.dma_start(offs_sb[:], offs)
         nc.scalar.dma_start(kn_sb[KN_ROW:P, :], kn[0:1, :])
-        nc.scalar.dma_start(qn_rows[P - B : P, :], qn.rearrange("b q o -> b (q o)"))
-        early = []
-        for t in range(2):
-            raw = sb.tile([P, POOL], F32, name=f"early{t}")
-            nc.sync.dma_start(raw[:], q_rows[:, t, :])
-            early.append(raw)
-        nc.sync.dma_start(ks_sb[0:P:8, :].bitcast(I32), k_scales[0].bitcast(I32))
+        nc.scalar.dma_start(qn_rows[QN_ROW:P, :], qn.rearrange("b q o -> b (q o)"))
+        half = POOL // 2
+        raw0 = sb.tile([P, POOL], F32, name="raw0")
+        raw1 = [sb.tile([P, half], F32, name=f"raw1_{h}") for h in range(2)]
+        nc.sync.dma_start(raw0[:], q_planes[:, 0, :])
         nc.sync.dma_start(offq_sb[:], offq)
+        nc.sync.dma_start(raw1[0][:], q_planes[:, 1, :half])
+        nc.sync.dma_start(ks_sb[0:P:8, :].bitcast(I32), k_scales[0].bitcast(I32))
         nc.sync.dma_start(kw_sb[:], k_words[0].rearrange("p n t -> p (n t)").bitcast(I32))
-        late = []
-        for t in (2, 3):
-            raw = sb.tile([P, POOL], F32, name=f"late{t}", align_bytes=64)
-            nc.sync.dma_start(raw[:], q_rows[:, t, :])
-            late.append(raw)
+        nc.sync.dma_start(raw1[1][:], q_planes[:, 1, half:])
+        raw2 = sb.tile([P, POOL], F32, name="raw2", align_bytes=64)
+        nc.sync.dma_start(raw2[:], q_planes[:, 2, :])
+        raw3 = sb.tile([P, POOL], F32, name="raw3", align_bytes=64)
+        nc.sync.dma_start(raw3[:], q_planes[:, 3, :])
 
-        planes = [sb.tile([P, POOL], BF16, name=f"plane{t}") for t in range(2)]
-        for t in range(2):
-            nc.scalar.activation(planes[t][:], early[t][:], COPY)
+        rounded = [sb.tile([P, POOL], BF16, name=f"rounded{t}") for t in range(2)]
+        nc.scalar.activation(rounded[0][:], raw0[:], COPY)
+        nc.scalar.activation(rounded[1][:, :half], raw1[0][:], COPY)
         q_g = sb.tile([P, B * NQ, 4], BF16, name="q_g", align_bytes=64)
-        for t in range(2):
-            nc.scalar.activation(q_g[:, :, t], planes[t][:].indirect(offq_sb[:]), COPY)
+        nc.scalar.activation(q_g[:, :, 0], rounded[0][:].indirect(offq_sb[:]), COPY)
+        nc.scalar.activation(rounded[1][:, half:], raw1[1][:], COPY)
+        nc.scalar.activation(q_g[:, :, 1], rounded[1][:].indirect(offq_sb[:]), COPY)
 
         kn_g = sb.tile([P, B * N], F32, name="kn_g")
         nc.vector.tensor_copy(kn_g[:], kn_sb[:].indirect(offs_sb[:]))
         ks_g = sb.tile([P, B * N], U8, name="ks_g", align_bytes=64)
         nc.vector.tensor_copy(ks_g[:], ks_sb[:].indirect(offs_sb[:]))
         for r in range(4):
-            nc.sync.dma_start(ks_plane[r:P:32, :].bitcast(I32), ks_g[8 * r : P : 32, :].bitcast(I32))
-        held = B * N - PIECE
-        kw_g = sb.tile([P, held], U32, name="kw_g", align_bytes=64)
-        nc.vector.tensor_copy(kw_g[:], kw_sb[:].bitcast(U32).indirect(offs_sb[:, : held // 16]))
+            nc.sync.dma_start(ks_operand[r:P:32, :].bitcast(I32), ks_g[8 * r : P : 32, :].bitcast(I32))
+        last_slot0 = B * N - PIECE
+        kw_g = sb.tile([P, last_slot0], U32, name="kw_g", align_bytes=64)
+        nc.vector.tensor_copy(kw_g[:], kw_sb[:].bitcast(U32).indirect(offs_sb[:, : last_slot0 // LIST_ROWS]))
 
-        turned = [ps.tile([P, 4, P], F32, name=f"turned{b}", tag=f"bank{b}") for b in range(B)]
-        qn_turned = ps.tile([P, P], F32, name="qn_turned", tag="bank2")
+        kn_turned = [ps.tile([P, CHUNKS, P], F32, name=f"kn_turned{b}", tag=f"bank{b}") for b in range(B)]
+        qn_turned = ps.tile([P, P], F32, name="qn_turned", tag=f"bank{B}")
         nc.tensor.transpose(qn_turned[:], qn_rows[:], ident[:])
         for b in range(B):
-            for j in range(4):
-                nc.tensor.transpose(turned[b][:, j, :], kn_g[:, b * N + j * P : b * N + (j + 1) * P], ident[:])
-        cols = sb.tile([P, 4 * B + B], F32, name="cols", tag="plane0")
+            for j in range(CHUNKS):
+                nc.tensor.transpose(kn_turned[b][:, j, :], kn_g[:, b * N + j * P : b * N + (j + 1) * P], ident[:])
+        qn_col0 = B * CHUNKS
+        cols = sb.tile([P, qn_col0 + B], F32, name="cols", tag="rounded0")
         for b in range(B):
-            nc.scalar.activation(cols[:, 4 * b : 4 * b + 4], turned[b][:, :, KN_ROW], COPY)
-        nc.scalar.activation(cols[:, 4 * B : 4 * B + B], qn_turned[:, P - B : P], COPY)
+            nc.scalar.activation(cols[:, CHUNKS * b : CHUNKS * (b + 1)], kn_turned[b][:, :, KN_ROW], COPY)
+        nc.scalar.activation(cols[:, qn_col0 : qn_col0 + B], qn_turned[:, QN_ROW:P], COPY)
         spreads = [ps.tile([P, N], F32, name=f"spread{b}") for b in range(B)]
         for b in range(B):
-            for j in range(4):
-                column = cols[:, 4 * b + j : 4 * b + j + 1]
+            for j in range(CHUNKS):
+                column = cols[:, CHUNKS * b + j : CHUNKS * b + j + 1]
                 nc.tensor.transpose(spreads[b][:, j * P : (j + 1) * P], column.to_broadcast([P, P]), ident[:])
-
-        norms = sb.tile([P, B, N], F32, name="norms", tag="plane1")
+        norms = sb.tile([P, B, N], F32, name="norms", tag="rounded1")
         for b in range(B):
-            nc.scalar.activation(norms[:, b, :], spreads[b][:], IDENTITY, bias=cols[:, 4 * B + b : 4 * B + b + 1])
+            nc.scalar.activation(norms[:, b, :], spreads[b][:], IDENTITY, bias=cols[:, qn_col0 + b : qn_col0 + b + 1])
 
-        nc.vector.tensor_copy(q_g[:, :, 2], late[0][:].indirect(offq_sb[:]))
+        nc.vector.tensor_copy(q_g[:, :, 2], raw2[:].indirect(offq_sb[:]))
+        list_cols = NQ // LIST_ROWS
         for b in range(B):
-            nc.vector.tensor_copy(q_g[:, b * NQ : (b + 1) * NQ, 3], late[1][:].indirect(offq_sb[:, b * 8 : b * 8 + 8]))
+            offsets = offq_sb[:, b * list_cols : (b + 1) * list_cols]
+            nc.vector.tensor_copy(q_g[:, b * NQ : (b + 1) * NQ, 3], raw3[:].indirect(offsets))
         q_codes, q_scales = [], []
         for b in range(B):
             codes = sb.tile([P, NQ], U32, name=f"q_codes{b}", align_bytes=64)
             scales = sb.tile([P, NQ], U8, name=f"q_scales{b}", align_bytes=64)
-            nc.vector.quantize_mx(out=codes[:].bitcast(FP8X4), scales=scales[:], in_=q_g[:, b * NQ : (b + 1) * NQ, :].rearrange("p n t -> p (n t)"))
+            nc.vector.quantize_mx(
+                out=codes[:].bitcast(FP8X4),
+                scales=scales[:],
+                in_=q_g[:, b * NQ : (b + 1) * NQ, :].rearrange("p n t -> p (n t)"),
+            )
             q_codes.append(codes)
             q_scales.append(scales)
-        kw_last = sb.tile([P, PIECE], U32, name="kw_last", tag="late3", align_bytes=64)
-        nc.vector.tensor_copy(kw_last[:], kw_sb[:].bitcast(U32).indirect(offs_sb[:, held // 16 :]))
+        kw_last = sb.tile([P, PIECE], U32, name="kw_last", tag="raw3", align_bytes=64)
+        nc.vector.tensor_copy(kw_last[:], kw_sb[:].bitcast(U32).indirect(offs_sb[:, last_slot0 // LIST_ROWS :]))
 
         for i in range(B * N // PIECE):
-            s0 = i * PIECE
-            b, n0 = divmod(s0, N)
+            slot0 = i * PIECE
+            b, n0 = divmod(slot0, N)
+            words = kw_g[:, slot0 : slot0 + PIECE] if slot0 < last_slot0 else kw_last[:]
             acc = ps.tile([P, PIECE], F32, name=f"acc{i}", tag=f"bank{i}")
             nc.tensor.matmul_mx(
                 out=acc[:],
                 lhsT=q_codes[b][:].bitcast(FP8X4),
                 lhsT_scale=q_scales[b][:],
-                rhs=(kw_g[:, s0 : s0 + PIECE] if s0 < held else kw_last[:]).bitcast(FP8X4),
-                rhs_scale=ks_plane[:, s0 : s0 + PIECE],
+                rhs=words.bitcast(FP8X4),
+                rhs_scale=ks_operand[:, slot0 : slot0 + PIECE],
                 start=True,
                 stop=True,
             )

@@ -52,27 +52,22 @@ def tile_attend_lq_dist_topk_kernel(tc, qT, k_words, k_scales, kn, qn, offq, off
         nc.sync.dma_start(offs_sb[:], offs)
         nc.scalar.dma_start(kn_sb[KN_ROW:P, :], kn[0:1, :])
         nc.scalar.dma_start(qn_rows[QN_ROW:P, :], qn.rearrange("b q o -> b (q o)"))
-        half = POOL // 2
-        raw0 = sb.tile([P, POOL], F32, name="raw0")
-        raw1 = [sb.tile([P, half], F32, name=f"raw1_{h}") for h in range(2)]
-        nc.sync.dma_start(raw0[:], q_planes[:, 0, :])
+        raw = [sb.tile([P, POOL], F32, name=f"raw{t}") for t in range(4)]
+        nc.sync.dma_start(raw[2][:], q_planes[:, 2, :])
         nc.sync.dma_start(offq_sb[:], offq)
-        nc.sync.dma_start(raw1[0][:], q_planes[:, 1, :half])
         nc.sync.dma_start(ks_sb[0:P:8, :].bitcast(I32), k_scales[0].bitcast(I32))
+        nc.sync.dma_start(raw[0][:], q_planes[:, 0, :])
         nc.sync.dma_start(kw_sb[:], k_words[0].rearrange("p n t -> p (n t)").bitcast(I32))
-        nc.sync.dma_start(raw1[1][:], q_planes[:, 1, half:])
-        raw2 = sb.tile([P, POOL], F32, name="raw2", align_bytes=64)
-        nc.sync.dma_start(raw2[:], q_planes[:, 2, :])
-        raw3 = sb.tile([P, POOL], F32, name="raw3", align_bytes=64)
-        nc.sync.dma_start(raw3[:], q_planes[:, 3, :])
+        nc.sync.dma_start(raw[1][:], q_planes[:, 1, :])
+        nc.sync.dma_start(raw[3][:], q_planes[:, 3, :])
 
-        rounded = [sb.tile([P, POOL], BF16, name=f"rounded{t}") for t in range(2)]
-        nc.scalar.activation(rounded[0][:], raw0[:], COPY)
-        nc.scalar.activation(rounded[1][:, :half], raw1[0][:], COPY)
+        list_cols = NQ // LIST_ROWS
+        q_lists = [offq_sb[:, b * list_cols : (b + 1) * list_cols] for b in range(B)]
         q_g = sb.tile([P, B * NQ, 4], BF16, name="q_g", align_bytes=64)
-        nc.scalar.activation(q_g[:, :, 0], rounded[0][:].indirect(offq_sb[:]), COPY)
-        nc.scalar.activation(rounded[1][:, half:], raw1[1][:], COPY)
-        nc.scalar.activation(q_g[:, :, 1], rounded[1][:].indirect(offq_sb[:]), COPY)
+        rounded = [sb.tile([P, POOL], BF16, name=f"rounded{t}", align_bytes=64) for t in range(3)]
+        for t in (2, 0):
+            nc.scalar.activation(rounded[t][:], raw[t][:], COPY)
+            nc.scalar.activation(q_g[:, :, t], rounded[t][:].indirect(offq_sb[:]), COPY)
 
         kn_g = sb.tile([P, B * N], F32, name="kn_g")
         nc.vector.tensor_copy(kn_g[:], kn_sb[:].indirect(offs_sb[:]))
@@ -80,9 +75,8 @@ def tile_attend_lq_dist_topk_kernel(tc, qT, k_words, k_scales, kn, qn, offq, off
         nc.vector.tensor_copy(ks_g[:], ks_sb[:].indirect(offs_sb[:]))
         for r in range(4):
             nc.sync.dma_start(ks_operand[r:P:32, :].bitcast(I32), ks_g[8 * r : P : 32, :].bitcast(I32))
-        last_slot0 = B * N - PIECE
-        kw_g = sb.tile([P, last_slot0], U32, name="kw_g", align_bytes=64)
-        nc.vector.tensor_copy(kw_g[:], kw_sb[:].bitcast(U32).indirect(offs_sb[:, : last_slot0 // LIST_ROWS]))
+        kw_g = sb.tile([P, B * N], U32, name="kw_g", tag="rounded2", align_bytes=64)
+        nc.vector.tensor_copy(kw_g[:], kw_sb[:].bitcast(U32).indirect(offs_sb[:]))
 
         kn_turned = [ps.tile([P, CHUNKS, P], F32, name=f"kn_turned{b}", tag=f"bank{b}") for b in range(B)]
         qn_turned = ps.tile([P, P], F32, name="qn_turned", tag=f"bank{B}")
@@ -91,7 +85,7 @@ def tile_attend_lq_dist_topk_kernel(tc, qT, k_words, k_scales, kn, qn, offq, off
             for j in range(CHUNKS):
                 nc.tensor.transpose(kn_turned[b][:, j, :], kn_g[:, b * N + j * P : b * N + (j + 1) * P], ident[:])
         qn_col0 = B * CHUNKS
-        cols = sb.tile([P, qn_col0 + B], F32, name="cols", tag="rounded0")
+        cols = sb.tile([P, qn_col0 + B], F32, name="cols", tag="raw0")
         for b in range(B):
             nc.scalar.activation(cols[:, CHUNKS * b : CHUNKS * (b + 1)], kn_turned[b][:, :, KN_ROW], COPY)
         nc.scalar.activation(cols[:, qn_col0 : qn_col0 + B], qn_turned[:, QN_ROW:P], COPY)
@@ -100,15 +94,16 @@ def tile_attend_lq_dist_topk_kernel(tc, qT, k_words, k_scales, kn, qn, offq, off
             for j in range(CHUNKS):
                 column = cols[:, CHUNKS * b + j : CHUNKS * b + j + 1]
                 nc.tensor.transpose(spreads[b][:, j * P : (j + 1) * P], column.to_broadcast([P, P]), ident[:])
-        norms = sb.tile([P, B, N], F32, name="norms", tag="rounded1")
+        norms = [sb.tile([P, N], F32, name="norms0")]
+        nc.scalar.activation(norms[0][:], spreads[0][:], IDENTITY, bias=cols[:, qn_col0 : qn_col0 + 1])
+        nc.scalar.activation(rounded[1][:], raw[1][:], COPY)
         for b in range(B):
-            nc.scalar.activation(norms[:, b, :], spreads[b][:], IDENTITY, bias=cols[:, qn_col0 + b : qn_col0 + b + 1])
+            nc.scalar.activation(q_g[:, b * NQ : (b + 1) * NQ, 1], rounded[1][:].indirect(q_lists[b]), COPY)
+        norms.append(sb.tile([P, N], F32, name="norms1", tag="rounded1", align_bytes=64))
+        nc.scalar.activation(norms[1][:], spreads[1][:], IDENTITY, bias=cols[:, qn_col0 + 1 : qn_col0 + 2])
 
-        nc.vector.tensor_copy(q_g[:, :, 2], raw2[:].indirect(offq_sb[:]))
-        list_cols = NQ // LIST_ROWS
         for b in range(B):
-            offsets = offq_sb[:, b * list_cols : (b + 1) * list_cols]
-            nc.vector.tensor_copy(q_g[:, b * NQ : (b + 1) * NQ, 3], raw3[:].indirect(offsets))
+            nc.vector.tensor_copy(q_g[:, b * NQ : (b + 1) * NQ, 3], raw[3][:].indirect(q_lists[b]))
         q_codes, q_scales = [], []
         for b in range(B):
             codes = sb.tile([P, NQ], U32, name=f"q_codes{b}", align_bytes=64)
@@ -120,13 +115,10 @@ def tile_attend_lq_dist_topk_kernel(tc, qT, k_words, k_scales, kn, qn, offq, off
             )
             q_codes.append(codes)
             q_scales.append(scales)
-        kw_last = sb.tile([P, PIECE], U32, name="kw_last", tag="raw3", align_bytes=64)
-        nc.vector.tensor_copy(kw_last[:], kw_sb[:].bitcast(U32).indirect(offs_sb[:, last_slot0 // LIST_ROWS :]))
-
         for i in range(B * N // PIECE):
             slot0 = i * PIECE
             b, n0 = divmod(slot0, N)
-            words = kw_g[:, slot0 : slot0 + PIECE] if slot0 < last_slot0 else kw_last[:]
+            words = kw_g[:, slot0 : slot0 + PIECE]
             acc = ps.tile([P, PIECE], F32, name=f"acc{i}", tag=f"bank{i}")
             nc.tensor.matmul_mx(
                 out=acc[:],
@@ -138,5 +130,5 @@ def tile_attend_lq_dist_topk_kernel(tc, qT, k_words, k_scales, kn, qn, offq, off
                 stop=True,
             )
             res = sb.tile([P, PIECE], F32, name=f"res{i}")
-            nc.vector.scalar_tensor_tensor(res[:], acc[:], -2.0, norms[:, b, n0 : n0 + PIECE], MULT, ADD)
+            nc.vector.scalar_tensor_tensor(res[:], acc[:], -2.0, norms[b][:, n0 : n0 + PIECE], MULT, ADD)
             nc.sync.dma_start(out[b, :, n0 : n0 + PIECE], res[:])

@@ -22,6 +22,7 @@ ADD = mybir.AluOpType.add
 P = 128
 LIST_ROWS = 16
 KN_ROW = P - 1
+KS_ROW = P - D // 32
 QN_ROW = P - B
 CHUNKS = N // P
 PIECE = 256
@@ -42,11 +43,11 @@ def tile_attend_lq_dist_topk_kernel(tc, qT, k_words, k_scales, kn, qn, offq, off
         ks_operand = sb.tile([P, B * N], U8, name="ks_operand", align_bytes=64)
         ident = sb.tile([P, P], F32, name="ident")
 
-        nc.gpsimd.memset(ks_sb[:].bitcast(I32), 0)
         nc.vector.memset(kn_sb[0:KN_ROW, :], 0.0)
+        nc.vector.memset(ks_sb[0:KS_ROW, :].bitcast(I32), 0)
+        nc.vector.memset(ks_operand[:].bitcast(I32), 0)
+        nc.vector.memset(qn_rows[0:QN_ROW, :], 0.0)
         make_identity(nc, ident[:])
-        nc.gpsimd.memset(ks_operand[:].bitcast(I32), 0)
-        nc.gpsimd.memset(qn_rows[0:QN_ROW, :], 0.0)
 
         q_planes = qT.rearrange("(p t) c -> p t c", t=4)
         nc.sync.dma_start(offs_sb[:], offs)
@@ -55,7 +56,7 @@ def tile_attend_lq_dist_topk_kernel(tc, qT, k_words, k_scales, kn, qn, offq, off
         raw = [sb.tile([P, POOL], F32, name=f"raw{t}") for t in range(4)]
         nc.sync.dma_start(raw[2][:], q_planes[:, 2, :])
         nc.sync.dma_start(offq_sb[:], offq)
-        nc.sync.dma_start(ks_sb[0:P:8, :].bitcast(I32), k_scales[0].bitcast(I32))
+        nc.sync.dma_start(ks_sb[KS_ROW:P, :].bitcast(I32), k_scales[0].bitcast(I32))
         nc.sync.dma_start(raw[0][:], q_planes[:, 0, :])
         nc.sync.dma_start(kw_sb[:], k_words[0].rearrange("p n t -> p (n t)").bitcast(I32))
         nc.sync.dma_start(raw[1][:], q_planes[:, 1, :])
@@ -73,8 +74,9 @@ def tile_attend_lq_dist_topk_kernel(tc, qT, k_words, k_scales, kn, qn, offq, off
         nc.vector.tensor_copy(kn_g[:], kn_sb[:].indirect(offs_sb[:]))
         ks_g = sb.tile([P, B * N], U8, name="ks_g", align_bytes=64)
         nc.vector.tensor_copy(ks_g[:], ks_sb[:].indirect(offs_sb[:]))
-        for r in range(4):
-            nc.sync.dma_start(ks_operand[r:P:32, :].bitcast(I32), ks_g[8 * r : P : 32, :].bitcast(I32))
+        for Q in range(4):
+            rows = ks_g[KS_ROW + 4 * Q : KS_ROW + 4 * Q + 4, :]
+            nc.sync.dma_start(ks_operand[32 * Q : 32 * Q + 4, :].bitcast(I32), rows.bitcast(I32))
         kw_g = sb.tile([P, B * N], U32, name="kw_g", tag="rounded2", align_bytes=64)
         nc.vector.tensor_copy(kw_g[:], kw_sb[:].bitcast(U32).indirect(offs_sb[:]))
 

@@ -22,7 +22,7 @@ ADD = mybir.AluOpType.add
 P = 128
 LIST_ROWS = 16
 KN_ROW = P - 1
-KS_ROW = P - D // 32
+KS_ROW = 32
 QN_ROW = P - B
 CHUNKS = N // P
 PIECE = 256
@@ -43,8 +43,8 @@ def tile_attend_lq_dist_topk_kernel(tc, qT, k_words, k_scales, kn, qn, offq, off
         ks_operand = sb.tile([P, B * N], U8, name="ks_operand", align_bytes=64)
         ident = sb.tile([P, P], F32, name="ident")
 
+        nc.vector.memset(ks_sb[:].bitcast(I32), 0)
         nc.vector.memset(kn_sb[0:KN_ROW, :], 0.0)
-        nc.vector.memset(ks_sb[0:KS_ROW, :].bitcast(I32), 0)
         nc.vector.memset(ks_operand[:].bitcast(I32), 0)
         nc.vector.memset(qn_rows[0:QN_ROW, :], 0.0)
         make_identity(nc, ident[:])
@@ -56,7 +56,7 @@ def tile_attend_lq_dist_topk_kernel(tc, qT, k_words, k_scales, kn, qn, offq, off
         raw = [sb.tile([P, POOL], F32, name=f"raw{t}") for t in range(4)]
         nc.sync.dma_start(raw[2][:], q_planes[:, 2, :])
         nc.sync.dma_start(offq_sb[:], offq)
-        nc.sync.dma_start(ks_sb[KS_ROW:P, :].bitcast(I32), k_scales[0].bitcast(I32))
+        nc.sync.dma_start(ks_sb[KS_ROW : KS_ROW + 64 : 4, :].bitcast(I32), k_scales[0].bitcast(I32))
         nc.sync.dma_start(raw[0][:], q_planes[:, 0, :])
         nc.sync.dma_start(kw_sb[:], k_words[0].rearrange("p n t -> p (n t)").bitcast(I32))
         nc.sync.dma_start(raw[1][:], q_planes[:, 1, :])
@@ -75,7 +75,7 @@ def tile_attend_lq_dist_topk_kernel(tc, qT, k_words, k_scales, kn, qn, offq, off
         ks_g = sb.tile([P, B * N], U8, name="ks_g", align_bytes=64)
         nc.vector.tensor_copy(ks_g[:], ks_sb[:].indirect(offs_sb[:]))
         for Q in range(4):
-            rows = ks_g[KS_ROW + 4 * Q : KS_ROW + 4 * Q + 4, :]
+            rows = ks_g[KS_ROW + 16 * Q : KS_ROW + 16 * Q + 16 : 4, :]
             nc.sync.dma_start(ks_operand[32 * Q : 32 * Q + 4, :].bitcast(I32), rows.bitcast(I32))
         kw_g = sb.tile([P, B * N], U32, name="kw_g", tag="rounded2", align_bytes=64)
         nc.vector.tensor_copy(kw_g[:], kw_sb[:].bitcast(U32).indirect(offs_sb[:]))

@@ -32,6 +32,7 @@ def tile_attend_lq_dist_topk_kernel(tc, qT, k_words, k_scales, kn, qn, offq, off
     nc = tc.nc
     with ExitStack() as ctx:
         sb = ctx.enter_context(tc.tile_pool(name="sb", bufs=1))
+        shared = ctx.enter_context(tc.tile_pool(name="shared", bufs=1))
         ps = ctx.enter_context(tc.psum_pool(name="ps", bufs=1))
 
         offs_sb = sb.tile([P, B * N // LIST_ROWS], U16, name="offs_sb")
@@ -53,21 +54,23 @@ def tile_attend_lq_dist_topk_kernel(tc, qT, k_words, k_scales, kn, qn, offq, off
         nc.sync.dma_start(offs_sb[:], offs)
         nc.scalar.dma_start(kn_sb[KN_ROW:P, :], kn[0:1, :])
         nc.scalar.dma_start(qn_rows[QN_ROW:P, :], qn.rearrange("b q o -> b (q o)"))
-        raw = [sb.tile([P, POOL], F32, name=f"raw{t}") for t in range(4)]
+        raw = [sb.tile([P, POOL], F32, name=f"raw{t}", align_bytes=64) for t in range(4)]
         nc.sync.dma_start(raw[2][:], q_planes[:, 2, :])
+        nc.sync.dma_start(raw[0][:], q_planes[:, 0, :])
         nc.sync.dma_start(offq_sb[:], offq)
         nc.sync.dma_start(ks_sb[KS_ROW : KS_ROW + 64 : 4, :].bitcast(I32), k_scales[0].bitcast(I32))
-        nc.sync.dma_start(raw[0][:], q_planes[:, 0, :])
         nc.sync.dma_start(kw_sb[:], k_words[0].rearrange("p n t -> p (n t)").bitcast(I32))
         nc.sync.dma_start(raw[1][:], q_planes[:, 1, :])
         nc.sync.dma_start(raw[3][:], q_planes[:, 3, :])
 
         list_cols = NQ // LIST_ROWS
         q_lists = [offq_sb[:, b * list_cols : (b + 1) * list_cols] for b in range(B)]
-        q_g = sb.tile([P, B * NQ, 4], BF16, name="q_g", align_bytes=64)
-        rounded = [sb.tile([P, POOL], BF16, name=f"rounded{t}", align_bytes=64) for t in range(3)]
+        rounded = [sb.tile([P, POOL], BF16, name=f"rounded{t}", align_bytes=64) for t in range(2)]
+        rounded.append(shared.tile([P, POOL], BF16, name="rounded2", offset=0, align_bytes=64))
         for t in (2, 0):
             nc.scalar.activation(rounded[t][:], raw[t][:], COPY)
+        q_g = sb.tile([P, B * NQ, 4], BF16, name="q_g", align_bytes=64)
+        for t in (2, 0):
             nc.scalar.activation(q_g[:, :, t], rounded[t][:].indirect(offq_sb[:]), COPY)
 
         kn_g = sb.tile([P, B * N], F32, name="kn_g")
@@ -77,7 +80,7 @@ def tile_attend_lq_dist_topk_kernel(tc, qT, k_words, k_scales, kn, qn, offq, off
         for Q in range(4):
             rows = ks_g[KS_ROW + 16 * Q : KS_ROW + 16 * Q + 16 : 4, :]
             nc.sync.dma_start(ks_operand[32 * Q : 32 * Q + 4, :].bitcast(I32), rows.bitcast(I32))
-        kw_g = sb.tile([P, B * N], U32, name="kw_g", tag="rounded2", align_bytes=64)
+        kw_g = shared.tile([P, B * N], U32, name="kw_g", offset=1024, align_bytes=64)
         nc.vector.tensor_copy(kw_g[:], kw_sb[:].bitcast(U32).indirect(offs_sb[:]))
 
         kn_turned = [ps.tile([P, CHUNKS, P], F32, name=f"kn_turned{b}", tag=f"bank{b}") for b in range(B)]
@@ -87,7 +90,7 @@ def tile_attend_lq_dist_topk_kernel(tc, qT, k_words, k_scales, kn, qn, offq, off
             for j in range(CHUNKS):
                 nc.tensor.transpose(kn_turned[b][:, j, :], kn_g[:, b * N + j * P : b * N + (j + 1) * P], ident[:])
         qn_col0 = B * CHUNKS
-        cols = sb.tile([P, qn_col0 + B], F32, name="cols", tag="raw0")
+        cols = sb.tile([P, qn_col0 + B], F32, name="cols", tag="raw0", align_bytes=64)
         for b in range(B):
             nc.scalar.activation(cols[:, CHUNKS * b : CHUNKS * (b + 1)], kn_turned[b][:, :, KN_ROW], COPY)
         nc.scalar.activation(cols[:, qn_col0 : qn_col0 + B], qn_turned[:, QN_ROW:P], COPY)
@@ -96,13 +99,19 @@ def tile_attend_lq_dist_topk_kernel(tc, qT, k_words, k_scales, kn, qn, offq, off
             for j in range(CHUNKS):
                 column = cols[:, CHUNKS * b + j : CHUNKS * b + j + 1]
                 nc.tensor.transpose(spreads[b][:, j * P : (j + 1) * P], column.to_broadcast([P, P]), ident[:])
-        norms = [sb.tile([P, N], F32, name="norms0")]
-        nc.scalar.activation(norms[0][:], spreads[0][:], IDENTITY, bias=cols[:, qn_col0 : qn_col0 + 1])
+        norms = [sb.tile([P, PIECE], F32, name=f"norms{i}") for i in range(B * N // PIECE)]
+
+        def add_norms(i):
+            b, n0 = divmod(i * PIECE, N)
+            qn_col = cols[:, qn_col0 + b : qn_col0 + b + 1]
+            nc.scalar.activation(norms[i][:], spreads[b][:, n0 : n0 + PIECE], IDENTITY, bias=qn_col)
+
         nc.scalar.activation(rounded[1][:], raw[1][:], COPY)
+        add_norms(0)
         for b in range(B):
             nc.scalar.activation(q_g[:, b * NQ : (b + 1) * NQ, 1], rounded[1][:].indirect(q_lists[b]), COPY)
-        norms.append(sb.tile([P, N], F32, name="norms1", tag="rounded1", align_bytes=64))
-        nc.scalar.activation(norms[1][:], spreads[1][:], IDENTITY, bias=cols[:, qn_col0 + 1 : qn_col0 + 2])
+        for i in range(1, len(norms)):
+            add_norms(i)
 
         for b in range(B):
             nc.vector.tensor_copy(q_g[:, b * NQ : (b + 1) * NQ, 3], raw[3][:].indirect(q_lists[b]))
@@ -132,5 +141,5 @@ def tile_attend_lq_dist_topk_kernel(tc, qT, k_words, k_scales, kn, qn, offq, off
                 stop=True,
             )
             res = sb.tile([P, PIECE], F32, name=f"res{i}")
-            nc.vector.scalar_tensor_tensor(res[:], acc[:], -2.0, norms[b][:, n0 : n0 + PIECE], MULT, ADD)
+            nc.vector.scalar_tensor_tensor(res[:], acc[:], -2.0, norms[i][:], MULT, ADD)
             nc.sync.dma_start(out[b, :, n0 : n0 + PIECE], res[:])

@@ -26,6 +26,7 @@ KS_ROW = 32
 QN_ROW = P - B
 CHUNKS = N // P
 PIECE = 256
+WIDTHS = (128, 128, 256, 256, 256)
 
 
 def tile_attend_lq_dist_topk_kernel(tc, qT, k_words, k_scales, kn, qn, offq, offs, out):
@@ -57,8 +58,8 @@ def tile_attend_lq_dist_topk_kernel(tc, qT, k_words, k_scales, kn, qn, offq, off
         raw = [sb.tile([P, POOL], F32, name=f"raw{t}", align_bytes=64) for t in range(4)]
         nc.sync.dma_start(raw[2][:], q_planes[:, 2, :])
         nc.sync.dma_start(raw[0][:], q_planes[:, 0, :])
-        nc.sync.dma_start(offq_sb[:], offq)
         nc.sync.dma_start(ks_sb[KS_ROW : KS_ROW + 64 : 4, :].bitcast(I32), k_scales[0].bitcast(I32))
+        nc.sync.dma_start(offq_sb[:], offq)
         nc.sync.dma_start(kw_sb[:], k_words[0].rearrange("p n t -> p (n t)").bitcast(I32))
         nc.sync.dma_start(raw[1][:], q_planes[:, 1, :])
         nc.sync.dma_start(raw[3][:], q_planes[:, 3, :])
@@ -126,20 +127,21 @@ def tile_attend_lq_dist_topk_kernel(tc, qT, k_words, k_scales, kn, qn, offq, off
             )
             q_codes.append(codes)
             q_scales.append(scales)
-        for i in range(B * N // PIECE):
-            slot0 = i * PIECE
+        slot0 = 0
+        for i, width in enumerate(WIDTHS):
             b, n0 = divmod(slot0, N)
-            words = kw_g[:, slot0 : slot0 + PIECE]
-            acc = ps.tile([P, PIECE], F32, name=f"acc{i}", tag=f"bank{i}")
+            acc = ps.tile([P, width], F32, name=f"acc{i}", tag=f"bank{i}")
             nc.tensor.matmul_mx(
                 out=acc[:],
                 lhsT=q_codes[b][:].bitcast(FP8X4),
                 lhsT_scale=q_scales[b][:],
-                rhs=words.bitcast(FP8X4),
-                rhs_scale=ks_operand[:, slot0 : slot0 + PIECE],
+                rhs=kw_g[:, slot0 : slot0 + width].bitcast(FP8X4),
+                rhs_scale=ks_operand[:, slot0 : slot0 + width],
                 start=True,
                 stop=True,
             )
-            res = sb.tile([P, PIECE], F32, name=f"res{i}")
-            nc.vector.scalar_tensor_tensor(res[:], acc[:], -2.0, norms[i][:], MULT, ADD)
-            nc.sync.dma_start(out[b, :, n0 : n0 + PIECE], res[:])
+            res = sb.tile([P, width], F32, name=f"res{i}")
+            piece, at = divmod(slot0, PIECE)
+            nc.vector.scalar_tensor_tensor(res[:], acc[:], -2.0, norms[piece][:, at : at + width], MULT, ADD)
+            nc.sync.dma_start(out[b, :, n0 : n0 + width], res[:])
+            slot0 = slot0 + width

@@ -47,7 +47,6 @@ def tile_attend_lq_dist_topk_kernel(tc, qT, k_words, k_scales, kn, qn, offq, off
 
         nc.vector.memset(ks_sb[:].bitcast(I32), 0)
         nc.vector.memset(kn_sb[0:KN_ROW, :], 0.0)
-        nc.vector.memset(ks_operand[:].bitcast(I32), 0)
         nc.vector.memset(qn_rows[0:QN_ROW, :], 0.0)
         make_identity(nc, ident[:])
 
@@ -91,7 +90,7 @@ def tile_attend_lq_dist_topk_kernel(tc, qT, k_words, k_scales, kn, qn, offq, off
             for j in range(CHUNKS):
                 nc.tensor.transpose(kn_turned[b][:, j, :], kn_g[:, b * N + j * P : b * N + (j + 1) * P], ident[:])
         qn_col0 = B * CHUNKS
-        cols = sb.tile([P, qn_col0 + B], F32, name="cols", tag="raw0", align_bytes=64)
+        cols = shared.tile([P, qn_col0 + B], F32, name="cols", offset=0)
         for b in range(B):
             nc.scalar.activation(cols[:, CHUNKS * b : CHUNKS * (b + 1)], kn_turned[b][:, :, KN_ROW], COPY)
         nc.scalar.activation(cols[:, qn_col0 : qn_col0 + B], qn_turned[:, QN_ROW:P], COPY)
@@ -100,18 +99,17 @@ def tile_attend_lq_dist_topk_kernel(tc, qT, k_words, k_scales, kn, qn, offq, off
             for j in range(CHUNKS):
                 column = cols[:, CHUNKS * b + j : CHUNKS * b + j + 1]
                 nc.tensor.transpose(spreads[b][:, j * P : (j + 1) * P], column.to_broadcast([P, P]), ident[:])
-        norms = [sb.tile([P, PIECE], F32, name=f"norms{i}") for i in range(B * N // PIECE)]
 
         def add_norms(i):
             b, n0 = divmod(i * PIECE, N)
             qn_col = cols[:, qn_col0 + b : qn_col0 + b + 1]
-            nc.scalar.activation(norms[i][:], spreads[b][:, n0 : n0 + PIECE], IDENTITY, bias=qn_col)
+            nc.scalar.activation(norms[:, i * PIECE : (i + 1) * PIECE], spreads[b][:, n0 : n0 + PIECE], IDENTITY, bias=qn_col)
 
         nc.scalar.activation(rounded[1][:], raw[1][:], COPY)
-        add_norms(0)
         for b in range(B):
             nc.scalar.activation(q_g[:, b * NQ : (b + 1) * NQ, 1], rounded[1][:].indirect(q_lists[b]), COPY)
-        for i in range(1, len(norms)):
+        norms = sb.tile([P, B * N], F32, name="norms", tag="raw1", align_bytes=64)
+        for i in range(B * N // PIECE):
             add_norms(i)
 
         for b in range(B):
@@ -141,7 +139,6 @@ def tile_attend_lq_dist_topk_kernel(tc, qT, k_words, k_scales, kn, qn, offq, off
                 stop=True,
             )
             res = sb.tile([P, width], F32, name=f"res{i}")
-            piece, at = divmod(slot0, PIECE)
-            nc.vector.scalar_tensor_tensor(res[:], acc[:], -2.0, norms[piece][:, at : at + width], MULT, ADD)
+            nc.vector.scalar_tensor_tensor(res[:], acc[:], -2.0, norms[:, slot0 : slot0 + width], MULT, ADD)
             nc.sync.dma_start(out[b, :, n0 : n0 + width], res[:])
             slot0 = slot0 + width

@@ -41,7 +41,7 @@ def tile_attend_lq_dist_topk_kernel(tc, qT, k_words, k_scales, kn, qn, offq, off
         kn_sb = sb.tile([P, T], F32, name="kn_sb")
         ks_sb = sb.tile([P, T], U8, name="ks_sb", align_bytes=64)
         kw_sb = sb.tile([P, T], I32, name="kw_sb", align_bytes=64)
-        qn_rows = sb.tile([P, NQ], F32, name="qn_rows")
+        qn_rows = sb.tile([P, NQ], F32, name="qn_rows", align_bytes=64)
         ks_operand = sb.tile([P, B * N], U8, name="ks_operand", align_bytes=64)
         ident = sb.tile([P, P], F32, name="ident")
 
@@ -56,8 +56,8 @@ def tile_attend_lq_dist_topk_kernel(tc, qT, k_words, k_scales, kn, qn, offq, off
         nc.scalar.dma_start(qn_rows[QN_ROW:P, :], qn.rearrange("b q o -> b (q o)"))
         raw = [sb.tile([P, POOL], F32, name=f"raw{t}", align_bytes=64) for t in range(4)]
         nc.sync.dma_start(raw[2][:], q_planes[:, 2, :])
-        nc.sync.dma_start(raw[0][:], q_planes[:, 0, :])
         nc.sync.dma_start(ks_sb[KS_ROW : KS_ROW + 64 : 4, :].bitcast(I32), k_scales[0].bitcast(I32))
+        nc.sync.dma_start(raw[0][:], q_planes[:, 0, :])
         nc.sync.dma_start(offq_sb[:], offq)
         nc.sync.dma_start(kw_sb[:], k_words[0].rearrange("p n t -> p (n t)").bitcast(I32))
         nc.sync.dma_start(raw[1][:], q_planes[:, 1, :])
@@ -66,31 +66,31 @@ def tile_attend_lq_dist_topk_kernel(tc, qT, k_words, k_scales, kn, qn, offq, off
         list_cols = NQ // LIST_ROWS
         q_lists = [offq_sb[:, b * list_cols : (b + 1) * list_cols] for b in range(B)]
         rounded = [sb.tile([P, POOL], BF16, name=f"rounded{t}", align_bytes=64) for t in range(2)]
-        rounded.append(shared.tile([P, POOL], BF16, name="rounded2", offset=0, align_bytes=64))
+        rounded.append(shared.tile([P, POOL], BF16, name="rounded2", offset=4096, align_bytes=64))
         for t in (2, 0):
             nc.scalar.activation(rounded[t][:], raw[t][:], COPY)
         q_g = sb.tile([P, B * NQ, 4], BF16, name="q_g", align_bytes=64)
         for t in (2, 0):
             nc.scalar.activation(q_g[:, :, t], rounded[t][:].indirect(offq_sb[:]), COPY)
 
-        kn_g = sb.tile([P, B * N], F32, name="kn_g")
+        kn_g = shared.tile([P, B * N], F32, name="kn_g", offset=0)
         nc.vector.tensor_copy(kn_g[:], kn_sb[:].indirect(offs_sb[:]))
-        ks_g = sb.tile([P, B * N], U8, name="ks_g", align_bytes=64)
+        qn_turned = ps.tile([P, P], F32, name="qn_turned", tag=f"bank{B}")
+        nc.tensor.transpose(qn_turned[:], qn_rows[:], ident[:])
+        ks_g = sb.tile([P, B * N], U8, name="ks_g", tag="qn_rows", align_bytes=64)
         nc.vector.tensor_copy(ks_g[:], ks_sb[:].indirect(offs_sb[:]))
         for Q in range(4):
             rows = ks_g[KS_ROW + 16 * Q : KS_ROW + 16 * Q + 16 : 4, :]
             nc.sync.dma_start(ks_operand[32 * Q : 32 * Q + 4, :].bitcast(I32), rows.bitcast(I32))
-        kw_g = shared.tile([P, B * N], U32, name="kw_g", offset=1024, align_bytes=64)
-        nc.vector.tensor_copy(kw_g[:], kw_sb[:].bitcast(U32).indirect(offs_sb[:]))
 
         kn_turned = [ps.tile([P, CHUNKS, P], F32, name=f"kn_turned{b}", tag=f"bank{b}") for b in range(B)]
-        qn_turned = ps.tile([P, P], F32, name="qn_turned", tag=f"bank{B}")
-        nc.tensor.transpose(qn_turned[:], qn_rows[:], ident[:])
         for b in range(B):
             for j in range(CHUNKS):
                 nc.tensor.transpose(kn_turned[b][:, j, :], kn_g[:, b * N + j * P : b * N + (j + 1) * P], ident[:])
+        kw_g = shared.tile([P, B * N], U32, name="kw_g", offset=1024, align_bytes=64)
+        nc.vector.tensor_copy(kw_g[:], kw_sb[:].bitcast(U32).indirect(offs_sb[:]))
         qn_col0 = B * CHUNKS
-        cols = shared.tile([P, qn_col0 + B], F32, name="cols", offset=0)
+        cols = shared.tile([P, qn_col0 + B], F32, name="cols", offset=5120)
         for b in range(B):
             nc.scalar.activation(cols[:, CHUNKS * b : CHUNKS * (b + 1)], kn_turned[b][:, :, KN_ROW], COPY)
         nc.scalar.activation(cols[:, qn_col0 : qn_col0 + B], qn_turned[:, QN_ROW:P], COPY)

@@ -26,6 +26,7 @@ KS_ROW = 32
 QN_ROW = P - B
 CHUNKS = N // P
 PIECE = 256
+KN_BYTES = N * 4
 WIDTHS = (128, 128, 256, 256, 256)
 
 
@@ -44,87 +45,85 @@ def tile_attend_lq_dist_topk_kernel(tc, qT, k_words, k_scales, kn, qn, offq, off
         qn_rows = sb.tile([P, NQ], F32, name="qn_rows", align_bytes=64)
         ks_operand = sb.tile([P, B * N], U8, name="ks_operand", align_bytes=64)
         ident = sb.tile([P, P], F32, name="ident")
+        first = sb.tile([P, POOL], F32, name="first", align_bytes=64)
+        middle = sb.tile([P, 2 * POOL], F32, name="middle", align_bytes=64)
+        last = sb.tile([P, POOL], F32, name="last", align_bytes=64)
 
         nc.vector.memset(ks_sb[:].bitcast(I32), 0)
         nc.vector.memset(kn_sb[0:KN_ROW, :], 0.0)
-        nc.vector.memset(qn_rows[0:QN_ROW, :], 0.0)
         make_identity(nc, ident[:])
 
-        q_planes = qT.rearrange("(p t) c -> p t c", t=4)
+        q_rows = qT.rearrange("(p t) c -> p (t c)", t=4)
         nc.sync.dma_start(offs_sb[:], offs)
         nc.scalar.dma_start(kn_sb[KN_ROW:P, :], kn[0:1, :])
         nc.scalar.dma_start(qn_rows[QN_ROW:P, :], qn.rearrange("b q o -> b (q o)"))
-        raw = [sb.tile([P, POOL], F32, name=f"raw{t}", align_bytes=64) for t in range(4)]
-        nc.sync.dma_start(raw[2][:], q_planes[:, 2, :])
+        nc.sync.dma_start(first[:], q_rows[:, 0:POOL])
         nc.sync.dma_start(ks_sb[KS_ROW : KS_ROW + 64 : 4, :].bitcast(I32), k_scales[0].bitcast(I32))
-        nc.sync.dma_start(raw[0][:], q_planes[:, 0, :])
-        nc.sync.dma_start(offq_sb[:], offq)
         nc.sync.dma_start(kw_sb[:], k_words[0].rearrange("p n t -> p (n t)").bitcast(I32))
-        nc.sync.dma_start(raw[1][:], q_planes[:, 1, :])
-        nc.sync.dma_start(raw[3][:], q_planes[:, 3, :])
+        nc.sync.dma_start(offq_sb[:], offq)
+        nc.sync.dma_start(middle[:], q_rows[:, POOL : 3 * POOL])
+        nc.sync.dma_start(last[:], q_rows[:, 3 * POOL : 4 * POOL])
+        nc.scalar.activation(qn_rows[0:QN_ROW, :], kn_sb[0:QN_ROW, 0:NQ], COPY)
 
         list_cols = NQ // LIST_ROWS
         q_lists = [offq_sb[:, b * list_cols : (b + 1) * list_cols] for b in range(B)]
-        rounded = [sb.tile([P, POOL], BF16, name=f"rounded{t}", align_bytes=64) for t in range(2)]
-        rounded.append(shared.tile([P, POOL], BF16, name="rounded2", offset=4096, align_bytes=64))
-        for t in (2, 0):
-            nc.scalar.activation(rounded[t][:], raw[t][:], COPY)
-        q_g = sb.tile([P, B * NQ, 4], BF16, name="q_g", align_bytes=64)
-        for t in (2, 0):
-            nc.scalar.activation(q_g[:, :, t], rounded[t][:].indirect(offq_sb[:]), COPY)
+        slot_cols = N // LIST_ROWS
 
-        kn_g = shared.tile([P, B * N], F32, name="kn_g", offset=0)
-        nc.vector.tensor_copy(kn_g[:], kn_sb[:].indirect(offs_sb[:]))
-        qn_turned = ps.tile([P, P], F32, name="qn_turned", tag=f"bank{B}")
-        nc.tensor.transpose(qn_turned[:], qn_rows[:], ident[:])
-        ks_g = sb.tile([P, B * N], U8, name="ks_g", tag="qn_rows", align_bytes=64)
+        ks_g = sb.tile([P, B * N], U8, name="ks_g", align_bytes=64)
         nc.vector.tensor_copy(ks_g[:], ks_sb[:].indirect(offs_sb[:]))
         for Q in range(4):
             rows = ks_g[KS_ROW + 16 * Q : KS_ROW + 16 * Q + 16 : 4, :]
             nc.sync.dma_start(ks_operand[32 * Q : 32 * Q + 4, :].bitcast(I32), rows.bitcast(I32))
-
-        kn_turned = [ps.tile([P, CHUNKS, P], F32, name=f"kn_turned{b}", tag=f"bank{b}") for b in range(B)]
-        for b in range(B):
-            for j in range(CHUNKS):
-                nc.tensor.transpose(kn_turned[b][:, j, :], kn_g[:, b * N + j * P : b * N + (j + 1) * P], ident[:])
-        kw_g = shared.tile([P, B * N], U32, name="kw_g", offset=1024, align_bytes=64)
+        kw_g = sb.tile([P, B * N], U32, name="kw_g", align_bytes=64)
         nc.vector.tensor_copy(kw_g[:], kw_sb[:].bitcast(U32).indirect(offs_sb[:]))
-        qn_col0 = B * CHUNKS
-        cols = shared.tile([P, qn_col0 + B], F32, name="cols", offset=5120)
+
+        kn_g = [shared.tile([P, N], F32, name=f"kn_g{b}", offset=b * KN_BYTES) for b in range(B)]
         for b in range(B):
-            nc.scalar.activation(cols[:, CHUNKS * b : CHUNKS * (b + 1)], kn_turned[b][:, :, KN_ROW], COPY)
-        nc.scalar.activation(cols[:, qn_col0 : qn_col0 + B], qn_turned[:, QN_ROW:P], COPY)
+            nc.scalar.activation(kn_g[b][:], kn_sb[:].indirect(offs_sb[:, b * slot_cols : (b + 1) * slot_cols]), COPY)
+        qn_turned = ps.tile([P, P], F32, name="qn_turned", tag=f"bank{B}")
+        nc.tensor.transpose(qn_turned[:], qn_rows[:], ident[:])
+        qn_cols = sb.tile([P, B], F32, name="qn_cols")
+        nc.scalar.activation(qn_cols[:], qn_turned[:, QN_ROW:P], COPY)
+        cols = [sb.tile([P, CHUNKS], F32, name=f"cols{b}") for b in range(B)]
         spreads = [ps.tile([P, N], F32, name=f"spread{b}") for b in range(B)]
         for b in range(B):
+            kn_turned = ps.tile([P, CHUNKS, P], F32, name=f"kn_turned{b}", tag=f"bank{b}")
             for j in range(CHUNKS):
-                column = cols[:, CHUNKS * b + j : CHUNKS * b + j + 1]
-                nc.tensor.transpose(spreads[b][:, j * P : (j + 1) * P], column.to_broadcast([P, P]), ident[:])
-
-        def add_norms(i):
-            b, n0 = divmod(i * PIECE, N)
-            qn_col = cols[:, qn_col0 + b : qn_col0 + b + 1]
-            nc.scalar.activation(norms[:, i * PIECE : (i + 1) * PIECE], spreads[b][:, n0 : n0 + PIECE], IDENTITY, bias=qn_col)
-
-        nc.scalar.activation(rounded[1][:], raw[1][:], COPY)
+                nc.tensor.transpose(kn_turned[:, j, :], kn_g[b][:, j * P : (j + 1) * P], ident[:])
+            nc.scalar.activation(cols[b][:], kn_turned[:, :, KN_ROW], COPY)
         for b in range(B):
-            nc.scalar.activation(q_g[:, b * NQ : (b + 1) * NQ, 1], rounded[1][:].indirect(q_lists[b]), COPY)
-        norms = sb.tile([P, B * N], F32, name="norms", tag="raw1", align_bytes=64)
-        for i in range(B * N // PIECE):
-            add_norms(i)
+            for j in range(CHUNKS):
+                nc.tensor.transpose(spreads[b][:, j * P : (j + 1) * P], cols[b][:, j : j + 1].to_broadcast([P, P]), ident[:])
 
+        q_g = [sb.tile([P, NQ, 4], BF16, name=f"q_g{b}", align_bytes=64) for b in range(B)]
+        pair = shared.tile([P, 2, B * NQ], F32, name="pair", offset=KN_BYTES // 2)
+        nc.scalar.activation(pair[:, 0, :], first[:].indirect(offq_sb[:]), COPY)
         for b in range(B):
-            nc.vector.tensor_copy(q_g[:, b * NQ : (b + 1) * NQ, 3], raw[3][:].indirect(q_lists[b]))
-        q_codes, q_scales = [], []
+            queries = slice(b * NQ, (b + 1) * NQ)
+            nc.scalar.activation(pair[:, 1, queries], middle[:, 0:POOL].indirect(q_lists[b]), COPY)
+            nc.scalar.activation(q_g[b][:, :, 0:2], pair[:, :, queries].rearrange("p t n -> p n t"), COPY)
+        norms = [sb.tile([P, N], F32, name=f"norms{b}", align_bytes=64) for b in range(B)]
         for b in range(B):
-            codes = sb.tile([P, NQ], U32, name=f"q_codes{b}", align_bytes=64)
-            scales = sb.tile([P, NQ], U8, name=f"q_scales{b}", align_bytes=64)
+            for n0 in range(0, N, PIECE):
+                nc.scalar.activation(
+                    norms[b][:, n0 : n0 + PIECE], spreads[b][:, n0 : n0 + PIECE], IDENTITY, bias=qn_cols[:, b : b + 1]
+                )
+        for t, window in ((2, middle[:, POOL : 2 * POOL]), (3, last[:])):
+            for b in range(B):
+                nc.vector.tensor_copy(q_g[b][:, :, t], window.indirect(q_lists[b]))
+
+        q_codes = [sb.tile([P, NQ], U32, name=f"q_codes{b}", align_bytes=64) for b in range(B)]
+        q_scales = [sb.tile([P, NQ], U8, name=f"q_scales{b}", align_bytes=64) for b in range(B)]
+
+        def quantise(b):
             nc.vector.quantize_mx(
-                out=codes[:].bitcast(FP8X4),
-                scales=scales[:],
-                in_=q_g[:, b * NQ : (b + 1) * NQ, :].rearrange("p n t -> p (n t)"),
+                out=q_codes[b][:].bitcast(FP8X4),
+                scales=q_scales[b][:],
+                in_=q_g[b][:].rearrange("p n t -> p (n t)"),
             )
-            q_codes.append(codes)
-            q_scales.append(scales)
+
+        quantise(0)
+        quantise(1)
         slot0 = 0
         for i, width in enumerate(WIDTHS):
             b, n0 = divmod(slot0, N)
@@ -139,6 +138,6 @@ def tile_attend_lq_dist_topk_kernel(tc, qT, k_words, k_scales, kn, qn, offq, off
                 stop=True,
             )
             res = sb.tile([P, width], F32, name=f"res{i}")
-            nc.vector.scalar_tensor_tensor(res[:], acc[:], -2.0, norms[:, slot0 : slot0 + width], MULT, ADD)
+            nc.vector.scalar_tensor_tensor(res[:], acc[:], -2.0, norms[b][:, n0 : n0 + width], MULT, ADD)
             nc.sync.dma_start(out[b, :, n0 : n0 + width], res[:])
             slot0 = slot0 + width

@@ -77,7 +77,7 @@ def tile_attend_lq_dist_topk_kernel(tc, qT, k_words, k_scales, kn, qn, offq, off
         kw_g = sb.tile([P, B * N], U32, name="kw_g", align_bytes=64)
         nc.vector.tensor_copy(kw_g[:], kw_sb[:].bitcast(U32).indirect(offs_sb[:]))
 
-        kn_g = [shared.tile([P, N], F32, name=f"kn_g{b}", offset=b * KN_BYTES) for b in range(B)]
+        kn_g = [shared.tile([P, N], F32, name=f"kn_g{b}", offset=KN_BYTES // 2 + b * KN_BYTES) for b in range(B)]
         for b in range(B):
             nc.scalar.activation(kn_g[b][:], kn_sb[:].indirect(offs_sb[:, b * slot_cols : (b + 1) * slot_cols]), COPY)
         qn_turned = ps.tile([P, P], F32, name="qn_turned", tag=f"bank{B}")
@@ -96,21 +96,23 @@ def tile_attend_lq_dist_topk_kernel(tc, qT, k_words, k_scales, kn, qn, offq, off
                 nc.tensor.transpose(spreads[b][:, j * P : (j + 1) * P], cols[b][:, j : j + 1].to_broadcast([P, P]), ident[:])
 
         q_g = [sb.tile([P, NQ, 4], BF16, name=f"q_g{b}", align_bytes=64) for b in range(B)]
-        pair = shared.tile([P, 2, B * NQ], F32, name="pair", offset=KN_BYTES // 2)
-        nc.scalar.activation(pair[:, 0, :], first[:].indirect(offq_sb[:]), COPY)
+        low = shared.tile([P, 2, B * NQ], F32, name="low", offset=0)
+        high = shared.tile([P, 2, NQ], F32, name="high", offset=KN_BYTES)
+        nc.scalar.activation(low[:, 0, :], first[:].indirect(offq_sb[:]), COPY)
         for b in range(B):
-            queries = slice(b * NQ, (b + 1) * NQ)
-            nc.scalar.activation(pair[:, 1, queries], middle[:, 0:POOL].indirect(q_lists[b]), COPY)
-            nc.scalar.activation(q_g[b][:, :, 0:2], pair[:, :, queries].rearrange("p t n -> p n t"), COPY)
-        norms = [sb.tile([P, N], F32, name=f"norms{b}", align_bytes=64) for b in range(B)]
+            nc.scalar.activation(low[:, 1, b * NQ : (b + 1) * NQ], middle[:, 0:POOL].indirect(q_lists[b]), COPY)
+        nc.scalar.activation(high[:, 0, :], middle[:, POOL : 2 * POOL].indirect(q_lists[1]), COPY)
+        nc.scalar.activation(high[:, 1, :], last[:].indirect(q_lists[1]), COPY)
+        nc.vector.tensor_copy(q_g[0][:, :, 2], middle[:, POOL : 2 * POOL].indirect(q_lists[0]))
+        for b in range(B):
+            nc.vector.tensor_copy(q_g[b][:, :, 0:2], low[:, :, b * NQ : (b + 1) * NQ].rearrange("p t n -> p n t"))
+        nc.vector.tensor_copy(q_g[0][:, :, 3], last[:].indirect(q_lists[0]))
+        norms = sb.tile([P, B, N], F32, name="norms", tag="last", align_bytes=64)
         for b in range(B):
             for n0 in range(0, N, PIECE):
                 nc.scalar.activation(
-                    norms[b][:, n0 : n0 + PIECE], spreads[b][:, n0 : n0 + PIECE], IDENTITY, bias=qn_cols[:, b : b + 1]
+                    norms[:, b, n0 : n0 + PIECE], spreads[b][:, n0 : n0 + PIECE], IDENTITY, bias=qn_cols[:, b : b + 1]
                 )
-        for t, window in ((2, middle[:, POOL : 2 * POOL]), (3, last[:])):
-            for b in range(B):
-                nc.vector.tensor_copy(q_g[b][:, :, t], window.indirect(q_lists[b]))
 
         q_codes = [sb.tile([P, NQ], U32, name=f"q_codes{b}", align_bytes=64) for b in range(B)]
         q_scales = [sb.tile([P, NQ], U8, name=f"q_scales{b}", align_bytes=64) for b in range(B)]
@@ -123,6 +125,7 @@ def tile_attend_lq_dist_topk_kernel(tc, qT, k_words, k_scales, kn, qn, offq, off
             )
 
         quantise(0)
+        nc.vector.tensor_copy(q_g[1][:, :, 2:4], high[:].rearrange("p t n -> p n t"))
         quantise(1)
         slot0 = 0
         for i, width in enumerate(WIDTHS):
@@ -138,6 +141,6 @@ def tile_attend_lq_dist_topk_kernel(tc, qT, k_words, k_scales, kn, qn, offq, off
                 stop=True,
             )
             res = sb.tile([P, width], F32, name=f"res{i}")
-            nc.vector.scalar_tensor_tensor(res[:], acc[:], -2.0, norms[b][:, n0 : n0 + width], MULT, ADD)
+            nc.vector.scalar_tensor_tensor(res[:], acc[:], -2.0, norms[:, b, n0 : n0 + width], MULT, ADD)
             nc.sync.dma_start(out[b, :, n0 : n0 + width], res[:])
             slot0 = slot0 + width

@@ -46,7 +46,8 @@ def tile_attend_lq_dist_topk_kernel(tc, qT, k_words, k_scales, kn, qn, offq, off
         ks_operand = sb.tile([P, B * N], U8, name="ks_operand", align_bytes=64)
         ident = sb.tile([P, P], F32, name="ident")
         first = sb.tile([P, POOL], F32, name="first", align_bytes=64)
-        middle = sb.tile([P, 2 * POOL], F32, name="middle", align_bytes=64)
+        second = sb.tile([P, POOL], F32, name="second", align_bytes=64)
+        third = sb.tile([P, POOL], F32, name="third", align_bytes=64)
         last = sb.tile([P, POOL], F32, name="last", align_bytes=64)
 
         nc.vector.memset(ks_sb[:].bitcast(I32), 0)
@@ -61,7 +62,8 @@ def tile_attend_lq_dist_topk_kernel(tc, qT, k_words, k_scales, kn, qn, offq, off
         nc.sync.dma_start(ks_sb[KS_ROW : KS_ROW + 64 : 4, :].bitcast(I32), k_scales[0].bitcast(I32))
         nc.sync.dma_start(kw_sb[:], k_words[0].rearrange("p n t -> p (n t)").bitcast(I32))
         nc.sync.dma_start(offq_sb[:], offq)
-        nc.sync.dma_start(middle[:], q_rows[:, POOL : 3 * POOL])
+        nc.sync.dma_start(second[:], q_rows[:, POOL : 2 * POOL])
+        nc.sync.dma_start(third[:], q_rows[:, 2 * POOL : 3 * POOL])
         nc.sync.dma_start(last[:], q_rows[:, 3 * POOL : 4 * POOL])
         nc.scalar.activation(qn_rows[0:QN_ROW, :], kn_sb[0:QN_ROW, 0:NQ], COPY)
 
@@ -77,13 +79,14 @@ def tile_attend_lq_dist_topk_kernel(tc, qT, k_words, k_scales, kn, qn, offq, off
         kw_g = sb.tile([P, B * N], U32, name="kw_g", align_bytes=64)
         nc.vector.tensor_copy(kw_g[:], kw_sb[:].bitcast(U32).indirect(offs_sb[:]))
 
-        kn_g = [shared.tile([P, N], F32, name=f"kn_g{b}", offset=KN_BYTES // 2 + b * KN_BYTES) for b in range(B)]
+        kn_g = [shared.tile([P, N], F32, name=f"kn_g{b}", offset=b * KN_BYTES) for b in range(B)]
         for b in range(B):
             nc.scalar.activation(kn_g[b][:], kn_sb[:].indirect(offs_sb[:, b * slot_cols : (b + 1) * slot_cols]), COPY)
         qn_turned = ps.tile([P, P], F32, name="qn_turned", tag=f"bank{B}")
         nc.tensor.transpose(qn_turned[:], qn_rows[:], ident[:])
-        qn_cols = sb.tile([P, B], F32, name="qn_cols")
-        nc.scalar.activation(qn_cols[:], qn_turned[:, QN_ROW:P], COPY)
+        qn_cols = [shared.tile([P, 1], F32, name=f"qn_col{b}", offset=(B + b) * KN_BYTES) for b in range(B)]
+        for b in range(B):
+            nc.scalar.activation(qn_cols[b][:], qn_turned[:, QN_ROW + b : QN_ROW + b + 1], COPY)
         cols = [sb.tile([P, CHUNKS], F32, name=f"cols{b}") for b in range(B)]
         spreads = [ps.tile([P, N], F32, name=f"spread{b}") for b in range(B)]
         for b in range(B):
@@ -97,22 +100,21 @@ def tile_attend_lq_dist_topk_kernel(tc, qT, k_words, k_scales, kn, qn, offq, off
 
         q_g = [sb.tile([P, NQ, 4], BF16, name=f"q_g{b}", align_bytes=64) for b in range(B)]
         low = shared.tile([P, 2, B * NQ], F32, name="low", offset=0)
-        high = shared.tile([P, 2, NQ], F32, name="high", offset=KN_BYTES)
+        high = shared.tile([P, 2, NQ], F32, name="high", offset=B * KN_BYTES - KN_BYTES // 4)
         nc.scalar.activation(low[:, 0, :], first[:].indirect(offq_sb[:]), COPY)
-        for b in range(B):
-            nc.scalar.activation(low[:, 1, b * NQ : (b + 1) * NQ], middle[:, 0:POOL].indirect(q_lists[b]), COPY)
-        nc.scalar.activation(high[:, 0, :], middle[:, POOL : 2 * POOL].indirect(q_lists[1]), COPY)
+        nc.scalar.activation(low[:, 1, :], second[:].indirect(offq_sb[:]), COPY)
+        norms = [
+            sb.tile([P, N], F32, name="norms0", align_bytes=64),
+            sb.tile([P, N], F32, name="norms1", tag="last", align_bytes=64),
+        ]
+        nc.scalar.activation(norms[0][:], spreads[0][:], IDENTITY, bias=qn_cols[0][:])
+        nc.scalar.activation(high[:, 0, :], third[:].indirect(q_lists[1]), COPY)
         nc.scalar.activation(high[:, 1, :], last[:].indirect(q_lists[1]), COPY)
-        nc.vector.tensor_copy(q_g[0][:, :, 2], middle[:, POOL : 2 * POOL].indirect(q_lists[0]))
+        nc.vector.tensor_copy(q_g[0][:, :, 2], third[:].indirect(q_lists[0]))
         for b in range(B):
             nc.vector.tensor_copy(q_g[b][:, :, 0:2], low[:, :, b * NQ : (b + 1) * NQ].rearrange("p t n -> p n t"))
         nc.vector.tensor_copy(q_g[0][:, :, 3], last[:].indirect(q_lists[0]))
-        norms = sb.tile([P, B, N], F32, name="norms", tag="last", align_bytes=64)
-        for b in range(B):
-            for n0 in range(0, N, PIECE):
-                nc.scalar.activation(
-                    norms[:, b, n0 : n0 + PIECE], spreads[b][:, n0 : n0 + PIECE], IDENTITY, bias=qn_cols[:, b : b + 1]
-                )
+        nc.scalar.activation(norms[1][:], spreads[1][:], IDENTITY, bias=qn_cols[1][:])
 
         q_codes = [sb.tile([P, NQ], U32, name=f"q_codes{b}", align_bytes=64) for b in range(B)]
         q_scales = [sb.tile([P, NQ], U8, name=f"q_scales{b}", align_bytes=64) for b in range(B)]
@@ -141,6 +143,6 @@ def tile_attend_lq_dist_topk_kernel(tc, qT, k_words, k_scales, kn, qn, offq, off
                 stop=True,
             )
             res = sb.tile([P, width], F32, name=f"res{i}")
-            nc.vector.scalar_tensor_tensor(res[:], acc[:], -2.0, norms[:, b, n0 : n0 + width], MULT, ADD)
+            nc.vector.scalar_tensor_tensor(res[:], acc[:], -2.0, norms[b][:, n0 : n0 + width], MULT, ADD)
             nc.sync.dma_start(out[b, :, n0 : n0 + width], res[:])
             slot0 = slot0 + width

@@ -45,8 +45,7 @@ def tile_attend_lq_dist_topk_kernel(tc, qT, k_words, k_scales, kn, qn, offq, off
         qn_rows = sb.tile([P, NQ], F32, name="qn_rows", align_bytes=64)
         ks_operand = sb.tile([P, B * N], U8, name="ks_operand", align_bytes=64)
         ident = sb.tile([P, P], F32, name="ident")
-        first = sb.tile([P, POOL], F32, name="first", align_bytes=64)
-        second = sb.tile([P, POOL], F32, name="second", align_bytes=64)
+        early = sb.tile([P, 2 * POOL], F32, name="early", align_bytes=64)
         third = sb.tile([P, POOL], F32, name="third", align_bytes=64)
         last = sb.tile([P, POOL], F32, name="last", align_bytes=64)
 
@@ -58,11 +57,11 @@ def tile_attend_lq_dist_topk_kernel(tc, qT, k_words, k_scales, kn, qn, offq, off
         nc.sync.dma_start(offs_sb[:], offs)
         nc.scalar.dma_start(kn_sb[KN_ROW:P, :], kn[0:1, :])
         nc.scalar.dma_start(qn_rows[QN_ROW:P, :], qn.rearrange("b q o -> b (q o)"))
-        nc.sync.dma_start(first[:], q_rows[:, 0:POOL])
+        nc.sync.dma_start(early[:, 0 : POOL // 2], q_rows[:, 0 : POOL // 2])
         nc.sync.dma_start(ks_sb[KS_ROW : KS_ROW + 64 : 4, :].bitcast(I32), k_scales[0].bitcast(I32))
         nc.sync.dma_start(kw_sb[:], k_words[0].rearrange("p n t -> p (n t)").bitcast(I32))
         nc.sync.dma_start(offq_sb[:], offq)
-        nc.sync.dma_start(second[:], q_rows[:, POOL : 2 * POOL])
+        nc.sync.dma_start(early[:, POOL // 2 : 2 * POOL], q_rows[:, POOL // 2 : 2 * POOL])
         nc.sync.dma_start(third[:], q_rows[:, 2 * POOL : 3 * POOL])
         nc.sync.dma_start(last[:], q_rows[:, 3 * POOL : 4 * POOL])
         nc.scalar.activation(qn_rows[0:QN_ROW, :], kn_sb[0:QN_ROW, 0:NQ], COPY)
@@ -84,9 +83,8 @@ def tile_attend_lq_dist_topk_kernel(tc, qT, k_words, k_scales, kn, qn, offq, off
             nc.scalar.activation(kn_g[b][:], kn_sb[:].indirect(offs_sb[:, b * slot_cols : (b + 1) * slot_cols]), COPY)
         qn_turned = ps.tile([P, P], F32, name="qn_turned", tag=f"bank{B}")
         nc.tensor.transpose(qn_turned[:], qn_rows[:], ident[:])
-        qn_cols = [shared.tile([P, 1], F32, name=f"qn_col{b}", offset=(B + b) * KN_BYTES) for b in range(B)]
-        for b in range(B):
-            nc.scalar.activation(qn_cols[b][:], qn_turned[:, QN_ROW + b : QN_ROW + b + 1], COPY)
+        qn_cols = sb.tile([P, B], F32, name="qn_cols")
+        nc.scalar.activation(qn_cols[:], qn_turned[:, QN_ROW:P], COPY)
         cols = [sb.tile([P, CHUNKS], F32, name=f"cols{b}") for b in range(B)]
         spreads = [ps.tile([P, N], F32, name=f"spread{b}") for b in range(B)]
         for b in range(B):
@@ -100,21 +98,21 @@ def tile_attend_lq_dist_topk_kernel(tc, qT, k_words, k_scales, kn, qn, offq, off
 
         q_g = [sb.tile([P, NQ, 4], BF16, name=f"q_g{b}", align_bytes=64) for b in range(B)]
         low = shared.tile([P, 2, B * NQ], F32, name="low", offset=0)
-        high = shared.tile([P, 2, NQ], F32, name="high", offset=B * KN_BYTES - KN_BYTES // 4)
-        nc.scalar.activation(low[:, 0, :], first[:].indirect(offq_sb[:]), COPY)
-        nc.scalar.activation(low[:, 1, :], second[:].indirect(offq_sb[:]), COPY)
-        norms = [
-            sb.tile([P, N], F32, name="norms0", align_bytes=64),
-            sb.tile([P, N], F32, name="norms1", tag="last", align_bytes=64),
-        ]
-        nc.scalar.activation(norms[0][:], spreads[0][:], IDENTITY, bias=qn_cols[0][:])
+        high = shared.tile([P, 2, NQ], F32, name="high", offset=KN_BYTES)
+        nc.scalar.activation(low[:, 0, :], early[:, 0:POOL].indirect(offq_sb[:]), COPY)
+        nc.scalar.activation(low[:, 1, :], early[:, POOL : 2 * POOL].indirect(offq_sb[:]), COPY)
         nc.scalar.activation(high[:, 0, :], third[:].indirect(q_lists[1]), COPY)
         nc.scalar.activation(high[:, 1, :], last[:].indirect(q_lists[1]), COPY)
         nc.vector.tensor_copy(q_g[0][:, :, 2], third[:].indirect(q_lists[0]))
         for b in range(B):
             nc.vector.tensor_copy(q_g[b][:, :, 0:2], low[:, :, b * NQ : (b + 1) * NQ].rearrange("p t n -> p n t"))
         nc.vector.tensor_copy(q_g[0][:, :, 3], last[:].indirect(q_lists[0]))
-        nc.scalar.activation(norms[1][:], spreads[1][:], IDENTITY, bias=qn_cols[1][:])
+        norms = sb.tile([P, B, N], F32, name="norms", tag="last", align_bytes=64)
+        for b in range(B):
+            for n0 in range(0, N, PIECE):
+                nc.scalar.activation(
+                    norms[:, b, n0 : n0 + PIECE], spreads[b][:, n0 : n0 + PIECE], IDENTITY, bias=qn_cols[:, b : b + 1]
+                )
 
         q_codes = [sb.tile([P, NQ], U32, name=f"q_codes{b}", align_bytes=64) for b in range(B)]
         q_scales = [sb.tile([P, NQ], U8, name=f"q_scales{b}", align_bytes=64) for b in range(B)]
@@ -143,6 +141,6 @@ def tile_attend_lq_dist_topk_kernel(tc, qT, k_words, k_scales, kn, qn, offq, off
                 stop=True,
             )
             res = sb.tile([P, width], F32, name=f"res{i}")
-            nc.vector.scalar_tensor_tensor(res[:], acc[:], -2.0, norms[b][:, n0 : n0 + width], MULT, ADD)
+            nc.vector.scalar_tensor_tensor(res[:], acc[:], -2.0, norms[:, b, n0 : n0 + width], MULT, ADD)
             nc.sync.dma_start(out[b, :, n0 : n0 + width], res[:])
             slot0 = slot0 + width

@@ -21,13 +21,14 @@ ADD = mybir.AluOpType.add
 
 P = 128
 LIST_ROWS = 16
-KN_ROW = P - 1
+HALF = T // 2
 KS_ROW = 32
 QN_ROW = P - B
 CHUNKS = N // P
 PIECE = 256
 KN_BYTES = N * 4
-WIDTHS = (128, 128, 256, 256, 256)
+STORES = (128, 128, 256, 256, 256)
+ACC_BANKS = 6
 
 
 def tile_attend_lq_dist_topk_kernel(tc, qT, k_words, k_scales, kn, qn, offq, offs, out):
@@ -50,12 +51,15 @@ def tile_attend_lq_dist_topk_kernel(tc, qT, k_words, k_scales, kn, qn, offq, off
         last = sb.tile([P, POOL], F32, name="last", align_bytes=64)
 
         nc.vector.memset(ks_sb[:].bitcast(I32), 0)
-        nc.vector.memset(kn_sb[0:KN_ROW, :], 0.0)
+        nc.vector.memset(kn_sb[0 : P - 1, 0:HALF], 0.0)
+        nc.vector.memset(kn_sb[0 : P // 2 - 1, HALF:T], 0.0)
+        nc.vector.memset(kn_sb[P // 2 : P, HALF:T], 0.0)
         make_identity(nc, ident[:])
 
         q_rows = qT.rearrange("(p t) c -> p (t c)", t=4)
         nc.sync.dma_start(offs_sb[:], offs)
-        nc.scalar.dma_start(kn_sb[KN_ROW:P, :], kn[0:1, :])
+        nc.scalar.dma_start(kn_sb[P - 1 : P, 0:HALF], kn[0:1, 0:HALF])
+        nc.scalar.dma_start(kn_sb[P // 2 - 1 : P // 2, HALF:T], kn[0:1, HALF:T])
         nc.scalar.dma_start(qn_rows[QN_ROW:P, :], qn.rearrange("b q o -> b (q o)"))
         nc.sync.dma_start(early[:, 0 : POOL // 2], q_rows[:, 0 : POOL // 2])
         nc.sync.dma_start(ks_sb[KS_ROW : KS_ROW + 64 : 4, :].bitcast(I32), k_scales[0].bitcast(I32))
@@ -85,16 +89,24 @@ def tile_attend_lq_dist_topk_kernel(tc, qT, k_words, k_scales, kn, qn, offq, off
         nc.tensor.transpose(qn_turned[:], qn_rows[:], ident[:])
         qn_cols = sb.tile([P, B], F32, name="qn_cols")
         nc.scalar.activation(qn_cols[:], qn_turned[:, QN_ROW:P], COPY)
-        cols = [sb.tile([P, CHUNKS], F32, name=f"cols{b}") for b in range(B)]
+        cols = [sb.tile([P, CHUNKS, 2], F32, name=f"cols{b}") for b in range(B)]
         spreads = [ps.tile([P, N], F32, name=f"spread{b}") for b in range(B)]
         for b in range(B):
             kn_turned = ps.tile([P, CHUNKS, P], F32, name=f"kn_turned{b}", tag=f"bank{b}")
             for j in range(CHUNKS):
                 nc.tensor.transpose(kn_turned[:, j, :], kn_g[b][:, j * P : (j + 1) * P], ident[:])
-            nc.scalar.activation(cols[b][:], kn_turned[:, :, KN_ROW], COPY)
+            nc.scalar.activation(cols[b][:], kn_turned[:, :, P // 2 - 1 : P : P // 2], COPY)
         for b in range(B):
             for j in range(CHUNKS):
-                nc.tensor.transpose(spreads[b][:, j * P : (j + 1) * P], cols[b][:, j : j + 1].to_broadcast([P, P]), ident[:])
+                for h in range(2):
+                    nc.tensor.matmul(
+                        spreads[b][:, j * P : (j + 1) * P],
+                        cols[b][:, j, h : h + 1].to_broadcast([P, P]),
+                        ident[:],
+                        start=(h == 0),
+                        stop=(h == 1),
+                        is_transpose=True,
+                    )
 
         q_g = [sb.tile([P, NQ, 4], BF16, name=f"q_g{b}", align_bytes=64) for b in range(B)]
         low = shared.tile([P, 2, B * NQ], F32, name="low", offset=0)
@@ -128,19 +140,23 @@ def tile_attend_lq_dist_topk_kernel(tc, qT, k_words, k_scales, kn, qn, offq, off
         nc.vector.tensor_copy(q_g[1][:, :, 2:4], high[:].rearrange("p t n -> p n t"))
         quantise(1)
         slot0 = 0
-        for i, width in enumerate(WIDTHS):
+        for i, width in enumerate(STORES):
             b, n0 = divmod(slot0, N)
-            acc = ps.tile([P, width], F32, name=f"acc{i}", tag=f"bank{i}")
-            nc.tensor.matmul_mx(
-                out=acc[:],
-                lhsT=q_codes[b][:].bitcast(FP8X4),
-                lhsT_scale=q_scales[b][:],
-                rhs=kw_g[:, slot0 : slot0 + width].bitcast(FP8X4),
-                rhs_scale=ks_operand[:, slot0 : slot0 + width],
-                start=True,
-                stop=True,
-            )
             res = sb.tile([P, width], F32, name=f"res{i}")
-            nc.vector.scalar_tensor_tensor(res[:], acc[:], -2.0, norms[:, b, n0 : n0 + width], MULT, ADD)
+            for c0 in range(0, width, P):
+                piece = (slot0 + c0) // P
+                acc = ps.tile([P, P], F32, name=f"acc{piece}", tag=f"bank{piece % ACC_BANKS}")
+                nc.tensor.matmul_mx(
+                    out=acc[:],
+                    lhsT=q_codes[b][:].bitcast(FP8X4),
+                    lhsT_scale=q_scales[b][:],
+                    rhs=kw_g[:, slot0 + c0 : slot0 + c0 + P].bitcast(FP8X4),
+                    rhs_scale=ks_operand[:, slot0 + c0 : slot0 + c0 + P],
+                    start=True,
+                    stop=True,
+                )
+                nc.vector.scalar_tensor_tensor(
+                    res[:, c0 : c0 + P], acc[:], -2.0, norms[:, b, n0 + c0 : n0 + c0 + P], MULT, ADD
+                )
             nc.sync.dma_start(out[b, :, n0 : n0 + width], res[:])
             slot0 = slot0 + width

@@ -57,11 +57,11 @@ def tile_attend_lq_dist_topk_kernel(tc, qT, k_words, k_scales, kn, qn, offq, off
         make_identity(nc, ident[:])
 
         q_rows = qT.rearrange("(p t) c -> p (t c)", t=4)
+        nc.sync.dma_start(early[:, 0 : POOL // 2], q_rows[:, 0 : POOL // 2])
         nc.sync.dma_start(offs_sb[:], offs)
         nc.scalar.dma_start(kn_sb[P - 1 : P, 0:HALF], kn[0:1, 0:HALF])
         nc.scalar.dma_start(kn_sb[P // 2 - 1 : P // 2, HALF:T], kn[0:1, HALF:T])
         nc.scalar.dma_start(qn_rows[QN_ROW:P, :], qn.rearrange("b q o -> b (q o)"))
-        nc.sync.dma_start(early[:, 0 : POOL // 2], q_rows[:, 0 : POOL // 2])
         nc.sync.dma_start(ks_sb[KS_ROW : KS_ROW + 64 : 4, :].bitcast(I32), k_scales[0].bitcast(I32))
         nc.sync.dma_start(kw_sb[:], k_words[0].rearrange("p n t -> p (n t)").bitcast(I32))
         nc.sync.dma_start(offq_sb[:], offq)

@@ -29,6 +29,7 @@ PIECE = 256
 KN_BYTES = N * 4
 STORES = (128, 128, 256, 256, 256)
 ACC_BANKS = 6
+ALIGN = 256
 
 
 def tile_attend_lq_dist_topk_kernel(tc, qT, k_words, k_scales, kn, qn, offq, offs, out):
@@ -38,17 +39,17 @@ def tile_attend_lq_dist_topk_kernel(tc, qT, k_words, k_scales, kn, qn, offq, off
         shared = ctx.enter_context(tc.tile_pool(name="shared", bufs=1))
         ps = ctx.enter_context(tc.psum_pool(name="ps", bufs=1))
 
-        offs_sb = sb.tile([P, B * N // LIST_ROWS], U16, name="offs_sb")
-        offq_sb = sb.tile([P, B * NQ // LIST_ROWS], U16, name="offq_sb")
-        kn_sb = sb.tile([P, T], F32, name="kn_sb")
-        ks_sb = sb.tile([P, T], U8, name="ks_sb", align_bytes=64)
-        kw_sb = sb.tile([P, T], I32, name="kw_sb", align_bytes=64)
-        qn_rows = sb.tile([P, NQ], F32, name="qn_rows", align_bytes=64)
-        ks_operand = sb.tile([P, B * N], U8, name="ks_operand", align_bytes=64)
+        offs_sb = sb.tile([P, B * N // LIST_ROWS], U16, name="offs_sb", align_bytes=ALIGN)
+        offq_sb = sb.tile([P, B * NQ // LIST_ROWS], U16, name="offq_sb", align_bytes=ALIGN)
+        kn_sb = sb.tile([P, T], F32, name="kn_sb", align_bytes=ALIGN)
+        ks_sb = sb.tile([P, T], U8, name="ks_sb", align_bytes=ALIGN)
+        kw_sb = sb.tile([P, T], I32, name="kw_sb", align_bytes=ALIGN)
+        qn_rows = sb.tile([P, NQ], F32, name="qn_rows", align_bytes=ALIGN)
+        ks_operand = sb.tile([P, B * N], U8, name="ks_operand", align_bytes=ALIGN)
         ident = sb.tile([P, P], F32, name="ident")
-        early = sb.tile([P, 2 * POOL], F32, name="early", align_bytes=64)
-        third = sb.tile([P, POOL], F32, name="third", align_bytes=64)
-        last = sb.tile([P, POOL], F32, name="last", align_bytes=64)
+        early = sb.tile([P, 2 * POOL], F32, name="early", align_bytes=ALIGN)
+        third = sb.tile([P, POOL], F32, name="third", align_bytes=ALIGN)
+        last = sb.tile([P, POOL], F32, name="last", align_bytes=ALIGN)
 
         nc.vector.memset(ks_sb[:].bitcast(I32), 0)
         nc.vector.memset(kn_sb[0 : P - 1, 0:HALF], 0.0)
@@ -74,12 +75,12 @@ def tile_attend_lq_dist_topk_kernel(tc, qT, k_words, k_scales, kn, qn, offq, off
         q_lists = [offq_sb[:, b * list_cols : (b + 1) * list_cols] for b in range(B)]
         slot_cols = N // LIST_ROWS
 
-        ks_g = sb.tile([P, B * N], U8, name="ks_g", align_bytes=64)
+        ks_g = sb.tile([P, B * N], U8, name="ks_g", align_bytes=ALIGN)
         nc.vector.tensor_copy(ks_g[:], ks_sb[:].indirect(offs_sb[:]))
         for Q in range(4):
             rows = ks_g[KS_ROW + 16 * Q : KS_ROW + 16 * Q + 16 : 4, :]
             nc.sync.dma_start(ks_operand[32 * Q : 32 * Q + 4, :].bitcast(I32), rows.bitcast(I32))
-        kw_g = sb.tile([P, B * N], U32, name="kw_g", align_bytes=64)
+        kw_g = sb.tile([P, B * N], U32, name="kw_g", align_bytes=ALIGN)
         nc.vector.tensor_copy(kw_g[:], kw_sb[:].bitcast(U32).indirect(offs_sb[:]))
 
         kn_g = [shared.tile([P, N], F32, name=f"kn_g{b}", offset=b * KN_BYTES) for b in range(B)]
@@ -108,26 +109,27 @@ def tile_attend_lq_dist_topk_kernel(tc, qT, k_words, k_scales, kn, qn, offq, off
                         is_transpose=True,
                     )
 
-        q_g = [sb.tile([P, NQ, 4], BF16, name=f"q_g{b}", align_bytes=64) for b in range(B)]
-        low = shared.tile([P, 2, B * NQ], F32, name="low", offset=0)
+        q_g = [sb.tile([P, NQ, 4], BF16, name=f"q_g{b}", align_bytes=ALIGN) for b in range(B)]
+        low = [shared.tile([P, 2, NQ], F32, name=f"low{b}", offset=b * KN_BYTES // 2) for b in range(B)]
         high = shared.tile([P, 2, NQ], F32, name="high", offset=KN_BYTES)
-        nc.scalar.activation(low[:, 0, :], early[:, 0:POOL].indirect(offq_sb[:]), COPY)
-        nc.scalar.activation(low[:, 1, :], early[:, POOL : 2 * POOL].indirect(offq_sb[:]), COPY)
+        for b in range(B):
+            for t in range(2):
+                nc.scalar.activation(low[b][:, t, :], early[:, t * POOL : (t + 1) * POOL].indirect(q_lists[b]), COPY)
         nc.scalar.activation(high[:, 0, :], third[:].indirect(q_lists[1]), COPY)
         nc.scalar.activation(high[:, 1, :], last[:].indirect(q_lists[1]), COPY)
         nc.vector.tensor_copy(q_g[0][:, :, 2], third[:].indirect(q_lists[0]))
-        for b in range(B):
-            nc.vector.tensor_copy(q_g[b][:, :, 0:2], low[:, :, b * NQ : (b + 1) * NQ].rearrange("p t n -> p n t"))
+        nc.vector.tensor_copy(q_g[0][:, :, 0:2], low[0][:].rearrange("p t n -> p n t"))
         nc.vector.tensor_copy(q_g[0][:, :, 3], last[:].indirect(q_lists[0]))
-        norms = sb.tile([P, B, N], F32, name="norms", tag="last", align_bytes=64)
+        nc.vector.tensor_copy(q_g[1][:, :, 0:2], low[1][:].rearrange("p t n -> p n t"))
+        norms = sb.tile([P, B, N], F32, name="norms", tag="last", align_bytes=ALIGN)
         for b in range(B):
             for n0 in range(0, N, PIECE):
                 nc.scalar.activation(
                     norms[:, b, n0 : n0 + PIECE], spreads[b][:, n0 : n0 + PIECE], IDENTITY, bias=qn_cols[:, b : b + 1]
                 )
 
-        q_codes = [sb.tile([P, NQ], U32, name=f"q_codes{b}", align_bytes=64) for b in range(B)]
-        q_scales = [sb.tile([P, NQ], U8, name=f"q_scales{b}", align_bytes=64) for b in range(B)]
+        q_codes = [sb.tile([P, NQ], U32, name=f"q_codes{b}", align_bytes=ALIGN) for b in range(B)]
+        q_scales = [sb.tile([P, NQ], U8, name=f"q_scales{b}", align_bytes=ALIGN) for b in range(B)]
 
         def quantise(b):
             nc.vector.quantize_mx(
@@ -142,7 +144,7 @@ def tile_attend_lq_dist_topk_kernel(tc, qT, k_words, k_scales, kn, qn, offq, off
         slot0 = 0
         for i, width in enumerate(STORES):
             b, n0 = divmod(slot0, N)
-            res = sb.tile([P, width], F32, name=f"res{i}")
+            res = sb.tile([P, width], F32, name=f"res{i}", align_bytes=ALIGN)
             for c0 in range(0, width, P):
                 piece = (slot0 + c0) // P
                 acc = ps.tile([P, P], F32, name=f"acc{piece}", tag=f"bank{piece % ACC_BANKS}")

@@ -21,7 +21,6 @@ ADD = mybir.AluOpType.add
 
 P = 128
 LIST_ROWS = 16
-HALF = T // 2
 KS_ROW = 32
 QN_ROW = P - B
 CHUNKS = N // P
@@ -52,16 +51,13 @@ def tile_attend_lq_dist_topk_kernel(tc, qT, k_words, k_scales, kn, qn, offq, off
         last = sb.tile([P, POOL], F32, name="last", align_bytes=ALIGN)
 
         nc.vector.memset(ks_sb[:].bitcast(I32), 0)
-        nc.vector.memset(kn_sb[0 : P - 1, 0:HALF], 0.0)
-        nc.vector.memset(kn_sb[0 : P // 2 - 1, HALF:T], 0.0)
-        nc.vector.memset(kn_sb[P // 2 : P, HALF:T], 0.0)
+        nc.vector.memset(kn_sb[0 : P - 1, :], 0.0)
         make_identity(nc, ident[:])
 
         q_rows = qT.rearrange("(p t) c -> p (t c)", t=4)
         nc.sync.dma_start(early[:, 0 : POOL // 2], q_rows[:, 0 : POOL // 2])
         nc.sync.dma_start(offs_sb[:], offs)
-        nc.scalar.dma_start(kn_sb[P - 1 : P, 0:HALF], kn[0:1, 0:HALF])
-        nc.scalar.dma_start(kn_sb[P // 2 - 1 : P // 2, HALF:T], kn[0:1, HALF:T])
+        nc.scalar.dma_start(kn_sb[P - 1 : P, :], kn[0:1, :])
         nc.scalar.dma_start(qn_rows[QN_ROW:P, :], qn.rearrange("b q o -> b (q o)"))
         nc.sync.dma_start(ks_sb[KS_ROW : KS_ROW + 64 : 4, :].bitcast(I32), k_scales[0].bitcast(I32))
         nc.sync.dma_start(kw_sb[:], k_words[0].rearrange("p n t -> p (n t)").bitcast(I32))
@@ -90,24 +86,16 @@ def tile_attend_lq_dist_topk_kernel(tc, qT, k_words, k_scales, kn, qn, offq, off
         nc.tensor.transpose(qn_turned[:], qn_rows[:], ident[:])
         qn_cols = sb.tile([P, B], F32, name="qn_cols")
         nc.scalar.activation(qn_cols[:], qn_turned[:, QN_ROW:P], COPY)
-        cols = [sb.tile([P, CHUNKS, 2], F32, name=f"cols{b}") for b in range(B)]
+        cols = [sb.tile([P, CHUNKS], F32, name=f"cols{b}") for b in range(B)]
         spreads = [ps.tile([P, N], F32, name=f"spread{b}") for b in range(B)]
         for b in range(B):
             kn_turned = ps.tile([P, CHUNKS, P], F32, name=f"kn_turned{b}", tag=f"bank{b}")
             for j in range(CHUNKS):
                 nc.tensor.transpose(kn_turned[:, j, :], kn_g[b][:, j * P : (j + 1) * P], ident[:])
-            nc.scalar.activation(cols[b][:], kn_turned[:, :, P // 2 - 1 : P : P // 2], COPY)
+            nc.scalar.activation(cols[b][:], kn_turned[:, :, P - 1], COPY)
         for b in range(B):
             for j in range(CHUNKS):
-                for h in range(2):
-                    nc.tensor.matmul(
-                        spreads[b][:, j * P : (j + 1) * P],
-                        cols[b][:, j, h : h + 1].to_broadcast([P, P]),
-                        ident[:],
-                        start=(h == 0),
-                        stop=(h == 1),
-                        is_transpose=True,
-                    )
+                nc.tensor.transpose(spreads[b][:, j * P : (j + 1) * P], cols[b][:, j : j + 1].to_broadcast([P, P]), ident[:])
 
         q_g = [sb.tile([P, NQ, 4], BF16, name=f"q_g{b}", align_bytes=ALIGN) for b in range(B)]
         low = [shared.tile([P, 2, NQ], F32, name=f"low{b}", offset=b * KN_BYTES // 2) for b in range(B)]

@@ -29,6 +29,7 @@ KN_BYTES = N * 4
 STORES = (128, 128, 256, 256, 256)
 ACC_BANKS = 6
 ALIGN = 256
+HEAD = 3 * POOL // 4
 
 
 def tile_attend_lq_dist_topk_kernel(tc, qT, k_words, k_scales, kn, qn, offq, offs, out):
@@ -55,14 +56,14 @@ def tile_attend_lq_dist_topk_kernel(tc, qT, k_words, k_scales, kn, qn, offq, off
         make_identity(nc, ident[:])
 
         q_rows = qT.rearrange("(p t) c -> p (t c)", t=4)
-        nc.sync.dma_start(early[:, 0 : POOL // 2], q_rows[:, 0 : POOL // 2])
+        nc.sync.dma_start(early[:, 0:HEAD], q_rows[:, 0:HEAD])
         nc.sync.dma_start(offs_sb[:], offs)
         nc.scalar.dma_start(kn_sb[P - 1 : P, :], kn[0:1, :])
         nc.scalar.dma_start(qn_rows[QN_ROW:P, :], qn.rearrange("b q o -> b (q o)"))
         nc.sync.dma_start(ks_sb[KS_ROW : KS_ROW + 64 : 4, :].bitcast(I32), k_scales[0].bitcast(I32))
         nc.sync.dma_start(kw_sb[:], k_words[0].rearrange("p n t -> p (n t)").bitcast(I32))
         nc.sync.dma_start(offq_sb[:], offq)
-        nc.sync.dma_start(early[:, POOL // 2 : 2 * POOL], q_rows[:, POOL // 2 : 2 * POOL])
+        nc.sync.dma_start(early[:, HEAD : 2 * POOL], q_rows[:, HEAD : 2 * POOL])
         nc.sync.dma_start(third[:], q_rows[:, 2 * POOL : 3 * POOL])
         nc.sync.dma_start(last[:], q_rows[:, 3 * POOL : 4 * POOL])
         nc.scalar.activation(qn_rows[0:QN_ROW, :], kn_sb[0:QN_ROW, 0:NQ], COPY)

@@ -27,7 +27,6 @@ CHUNKS = N // P
 PIECE = 256
 KN_BYTES = N * 4
 STORES = (128, 128, 256, 256, 256)
-ACC_BANKS = 6
 ALIGN = 256
 HEAD = 3 * POOL // 4
 
@@ -133,21 +132,17 @@ def tile_attend_lq_dist_topk_kernel(tc, qT, k_words, k_scales, kn, qn, offq, off
         slot0 = 0
         for i, width in enumerate(STORES):
             b, n0 = divmod(slot0, N)
+            acc = ps.tile([P, width], F32, name=f"acc{i}", tag=f"bank{i}")
+            nc.tensor.matmul_mx(
+                out=acc[:],
+                lhsT=q_codes[b][:].bitcast(FP8X4),
+                lhsT_scale=q_scales[b][:],
+                rhs=kw_g[:, slot0 : slot0 + width].bitcast(FP8X4),
+                rhs_scale=ks_operand[:, slot0 : slot0 + width],
+                start=True,
+                stop=True,
+            )
             res = sb.tile([P, width], F32, name=f"res{i}", align_bytes=ALIGN)
-            for c0 in range(0, width, P):
-                piece = (slot0 + c0) // P
-                acc = ps.tile([P, P], F32, name=f"acc{piece}", tag=f"bank{piece % ACC_BANKS}")
-                nc.tensor.matmul_mx(
-                    out=acc[:],
-                    lhsT=q_codes[b][:].bitcast(FP8X4),
-                    lhsT_scale=q_scales[b][:],
-                    rhs=kw_g[:, slot0 + c0 : slot0 + c0 + P].bitcast(FP8X4),
-                    rhs_scale=ks_operand[:, slot0 + c0 : slot0 + c0 + P],
-                    start=True,
-                    stop=True,
-                )
-                nc.vector.scalar_tensor_tensor(
-                    res[:, c0 : c0 + P], acc[:], -2.0, norms[:, b, n0 + c0 : n0 + c0 + P], MULT, ADD
-                )
+            nc.vector.scalar_tensor_tensor(res[:], acc[:], -2.0, norms[:, b, n0 : n0 + width], MULT, ADD)
             nc.sync.dma_start(out[b, :, n0 : n0 + width], res[:])
             slot0 = slot0 + width

@@ -24,7 +24,7 @@ LIST_ROWS = 16
 KS_ROW = 32
 QN_ROW = P - B
 CHUNKS = N // P
-PIECE = 256
+NORMS = (128, 384, 512)
 KN_BYTES = N * 4
 STORES = (128, 128, 256, 256, 256)
 ALIGN = 256
@@ -58,7 +58,8 @@ def tile_attend_lq_dist_topk_kernel(tc, qT, k_words, k_scales, kn, qn, offq, off
         nc.sync.dma_start(early[:, 0:HEAD], q_rows[:, 0:HEAD])
         nc.sync.dma_start(offs_sb[:], offs)
         nc.scalar.dma_start(kn_sb[P - 1 : P, :], kn[0:1, :])
-        nc.scalar.dma_start(qn_rows[QN_ROW:P, :], qn.rearrange("b q o -> b (q o)"))
+        for b in range(B):
+            nc.scalar.dma_start(qn_rows[QN_ROW + b : QN_ROW + b + 1, :], qn[b].rearrange("q o -> o q"))
         nc.sync.dma_start(ks_sb[KS_ROW : KS_ROW + 64 : 4, :].bitcast(I32), k_scales[0].bitcast(I32))
         nc.sync.dma_start(kw_sb[:], k_words[0].rearrange("p n t -> p (n t)").bitcast(I32))
         nc.sync.dma_start(offq_sb[:], offq)
@@ -73,9 +74,10 @@ def tile_attend_lq_dist_topk_kernel(tc, qT, k_words, k_scales, kn, qn, offq, off
 
         ks_g = sb.tile([P, B * N], U8, name="ks_g", align_bytes=ALIGN)
         nc.vector.tensor_copy(ks_g[:], ks_sb[:].indirect(offs_sb[:]))
-        for Q in range(4):
-            rows = ks_g[KS_ROW + 16 * Q : KS_ROW + 16 * Q + 16 : 4, :]
-            nc.sync.dma_start(ks_operand[32 * Q : 32 * Q + 4, :].bitcast(I32), rows.bitcast(I32))
+        moves = [(0, 0, B * N)] + [(Q, b * N, (b + 1) * N) for b in range(B) for Q in range(1, 4)]
+        for Q, c0, c1 in moves:
+            rows = ks_g[KS_ROW + 16 * Q : KS_ROW + 16 * Q + 16 : 4, c0:c1]
+            nc.sync.dma_start(ks_operand[32 * Q : 32 * Q + 4, c0:c1].bitcast(I32), rows.bitcast(I32))
         kw_g = sb.tile([P, B * N], U32, name="kw_g", align_bytes=ALIGN)
         nc.vector.tensor_copy(kw_g[:], kw_sb[:].bitcast(U32).indirect(offs_sb[:]))
 
@@ -87,16 +89,29 @@ def tile_attend_lq_dist_topk_kernel(tc, qT, k_words, k_scales, kn, qn, offq, off
         qn_cols = sb.tile([P, B], F32, name="qn_cols")
         nc.scalar.activation(qn_cols[:], qn_turned[:, QN_ROW:P], COPY)
         cols = [sb.tile([P, CHUNKS], F32, name=f"cols{b}") for b in range(B)]
-        spreads = [ps.tile([P, N], F32, name=f"spread{b}") for b in range(B)]
+        spreads = [ps.tile([P, w], F32, name=f"spread{h}", tag=f"spread{h}") for h, w in enumerate(NORMS)]
+        starts = [sum(NORMS[:h]) for h in range(len(NORMS))]
+
+        def piece(slot):
+            h = max(h for h in range(len(NORMS)) if starts[h] <= slot)
+            return h, slot - starts[h]
+
+        def spread(b, j):
+            h, c0 = piece(b * N + j * P)
+            nc.tensor.transpose(spreads[h][:, c0 : c0 + P], cols[b][:, j : j + 1].to_broadcast([P, P]), ident[:])
+
         for b in range(B):
-            kn_turned = ps.tile([P, CHUNKS, P], F32, name=f"kn_turned{b}", tag=f"bank{b}")
+            kn_turned = ps.tile([P, CHUNKS, P], F32, name=f"kn_turned{b}", tag="bank0")
             for j in range(CHUNKS):
                 nc.tensor.transpose(kn_turned[:, j, :], kn_g[b][:, j * P : (j + 1) * P], ident[:])
             nc.scalar.activation(cols[b][:], kn_turned[:, :, P - 1], COPY)
-        for b in range(B):
-            for j in range(CHUNKS):
-                nc.tensor.transpose(spreads[b][:, j * P : (j + 1) * P], cols[b][:, j : j + 1].to_broadcast([P, P]), ident[:])
+            if b == 0:
+                spread(0, 0)
+        for slot in range(P, B * N, P):
+            spread(slot // N, slot % N // P)
 
+        first_norms = sb.tile([P, NORMS[0]], F32, name="first_norms", align_bytes=ALIGN)
+        nc.vector.tensor_scalar_add(first_norms[:], spreads[0][:], qn_cols[:, 0:1])
         q_g = [sb.tile([P, NQ, 4], BF16, name=f"q_g{b}", align_bytes=ALIGN) for b in range(B)]
         low = [shared.tile([P, 2, NQ], F32, name=f"low{b}", offset=b * KN_BYTES // 2) for b in range(B)]
         high = shared.tile([P, 2, NQ], F32, name="high", offset=KN_BYTES)
@@ -109,12 +124,11 @@ def tile_attend_lq_dist_topk_kernel(tc, qT, k_words, k_scales, kn, qn, offq, off
         nc.vector.tensor_copy(q_g[0][:, :, 0:2], low[0][:].rearrange("p t n -> p n t"))
         nc.vector.tensor_copy(q_g[0][:, :, 3], last[:].indirect(q_lists[0]))
         nc.vector.tensor_copy(q_g[1][:, :, 0:2], low[1][:].rearrange("p t n -> p n t"))
-        norms = sb.tile([P, B, N], F32, name="norms", tag="last", align_bytes=ALIGN)
-        for b in range(B):
-            for n0 in range(0, N, PIECE):
-                nc.scalar.activation(
-                    norms[:, b, n0 : n0 + PIECE], spreads[b][:, n0 : n0 + PIECE], IDENTITY, bias=qn_cols[:, b : b + 1]
-                )
+        later_norms = sb.tile([P, B * N - NORMS[0]], F32, name="later_norms", tag="last", align_bytes=ALIGN)
+        norms = [first_norms[:], later_norms[:, 0 : NORMS[1]], later_norms[:, NORMS[1] :]]
+        for h in (2, 1):
+            b = starts[h] // N
+            nc.scalar.activation(norms[h], spreads[h][:], IDENTITY, bias=qn_cols[:, b : b + 1])
 
         q_codes = [sb.tile([P, NQ], U32, name=f"q_codes{b}", align_bytes=ALIGN) for b in range(B)]
         q_scales = [sb.tile([P, NQ], U8, name=f"q_scales{b}", align_bytes=ALIGN) for b in range(B)]
@@ -143,6 +157,7 @@ def tile_attend_lq_dist_topk_kernel(tc, qT, k_words, k_scales, kn, qn, offq, off
                 stop=True,
             )
             res = sb.tile([P, width], F32, name=f"res{i}", align_bytes=ALIGN)
-            nc.vector.scalar_tensor_tensor(res[:], acc[:], -2.0, norms[:, b, n0 : n0 + width], MULT, ADD)
+            h, c0 = piece(slot0)
+            nc.vector.scalar_tensor_tensor(res[:], acc[:], -2.0, norms[h][:, c0 : c0 + width], MULT, ADD)
             nc.sync.dma_start(out[b, :, n0 : n0 + width], res[:])
             slot0 = slot0 + width

@@ -58,8 +58,7 @@ def tile_attend_lq_dist_topk_kernel(tc, qT, k_words, k_scales, kn, qn, offq, off
         nc.sync.dma_start(early[:, 0:HEAD], q_rows[:, 0:HEAD])
         nc.sync.dma_start(offs_sb[:], offs)
         nc.scalar.dma_start(kn_sb[P - 1 : P, :], kn[0:1, :])
-        for b in range(B):
-            nc.scalar.dma_start(qn_rows[QN_ROW + b : QN_ROW + b + 1, :], qn[b].rearrange("q o -> o q"))
+        nc.scalar.dma_start(qn_rows[QN_ROW:P, :], qn.rearrange("b q o -> b (q o)"))
         nc.sync.dma_start(ks_sb[KS_ROW : KS_ROW + 64 : 4, :].bitcast(I32), k_scales[0].bitcast(I32))
         nc.sync.dma_start(kw_sb[:], k_words[0].rearrange("p n t -> p (n t)").bitcast(I32))
         nc.sync.dma_start(offq_sb[:], offq)
@@ -74,7 +73,8 @@ def tile_attend_lq_dist_topk_kernel(tc, qT, k_words, k_scales, kn, qn, offq, off
 
         ks_g = sb.tile([P, B * N], U8, name="ks_g", align_bytes=ALIGN)
         nc.vector.tensor_copy(ks_g[:], ks_sb[:].indirect(offs_sb[:]))
-        moves = [(0, 0, B * N)] + [(Q, b * N, (b + 1) * N) for b in range(B) for Q in range(1, 4)]
+        cut = B * N - STORES[-1]
+        moves = [(Q, c0, c1) for c0, c1 in ((0, cut), (cut, B * N)) for Q in range(4)]
         for Q, c0, c1 in moves:
             rows = ks_g[KS_ROW + 16 * Q : KS_ROW + 16 * Q + 16 : 4, c0:c1]
             nc.sync.dma_start(ks_operand[32 * Q : 32 * Q + 4, c0:c1].bitcast(I32), rows.bitcast(I32))

@@ -26,6 +26,7 @@ QN_ROW = P - B
 CHUNKS = N // P
 NORMS = (128, 384, 512)
 KN_BYTES = N * 4
+PRODUCT = 256
 STORES = (128, 128, 256, 256, 256)
 ALIGN = 256
 HEAD = 3 * POOL // 4
@@ -73,7 +74,7 @@ def tile_attend_lq_dist_topk_kernel(tc, qT, k_words, k_scales, kn, qn, offq, off
 
         ks_g = sb.tile([P, B * N], U8, name="ks_g", align_bytes=ALIGN)
         nc.vector.tensor_copy(ks_g[:], ks_sb[:].indirect(offs_sb[:]))
-        cut = B * N - STORES[-1]
+        cut = B * N - PRODUCT
         moves = [(Q, c0, c1) for c0, c1 in ((0, cut), (cut, B * N)) for Q in range(4)]
         for Q, c0, c1 in moves:
             rows = ks_g[KS_ROW + 16 * Q : KS_ROW + 16 * Q + 16 : 4, c0:c1]
@@ -143,21 +144,29 @@ def tile_attend_lq_dist_topk_kernel(tc, qT, k_words, k_scales, kn, qn, offq, off
         quantise(0)
         nc.vector.tensor_copy(q_g[1][:, :, 2:4], high[:].rearrange("p t n -> p n t"))
         quantise(1)
-        slot0 = 0
-        for i, width in enumerate(STORES):
-            b, n0 = divmod(slot0, N)
-            acc = ps.tile([P, width], F32, name=f"acc{i}", tag=f"bank{i}")
+        products = []
+        for i in range(B * N // PRODUCT):
+            slots = slice(i * PRODUCT, (i + 1) * PRODUCT)
+            b = slots.start // N
+            acc = ps.tile([P, PRODUCT], F32, name=f"acc{i}", tag=f"bank{i}")
             nc.tensor.matmul_mx(
                 out=acc[:],
                 lhsT=q_codes[b][:].bitcast(FP8X4),
                 lhsT_scale=q_scales[b][:],
-                rhs=kw_g[:, slot0 : slot0 + width].bitcast(FP8X4),
-                rhs_scale=ks_operand[:, slot0 : slot0 + width],
+                rhs=kw_g[:, slots].bitcast(FP8X4),
+                rhs_scale=ks_operand[:, slots],
                 start=True,
                 stop=True,
             )
-            res = sb.tile([P, width], F32, name=f"res{i}", align_bytes=ALIGN)
+            products.append(acc)
+        slot0 = 0
+        for i, width in enumerate(STORES):
+            b, n0 = divmod(slot0, N)
+            k, a0 = divmod(slot0, PRODUCT)
             h, c0 = piece(slot0)
-            nc.vector.scalar_tensor_tensor(res[:], acc[:], -2.0, norms[h][:, c0 : c0 + width], MULT, ADD)
+            res = sb.tile([P, width], F32, name=f"res{i}", align_bytes=ALIGN)
+            nc.vector.scalar_tensor_tensor(
+                res[:], products[k][:, a0 : a0 + width], -2.0, norms[h][:, c0 : c0 + width], MULT, ADD
+            )
             nc.sync.dma_start(out[b, :, n0 : n0 + width], res[:])
             slot0 = slot0 + width

from contextlib import ExitStack

import concourse.mybir as mybir
from concourse.masks import make_identity

B, N, T, D, NQ, POOL = 2, 512, 2048, 512, 128, 1024
FLOPS = 2 * B * NQ * N * D
BYTES = D * POOL * 4 + D * T + (D // 32) * T + T * 4 + B * NQ * 4 + 128 * (16 + 64) * 2 + B * NQ * N * 4

F32 = mybir.dt.float32
BF16 = mybir.dt.bfloat16
I32 = mybir.dt.int32
U32 = mybir.dt.uint32
U16 = mybir.dt.uint16
U8 = mybir.dt.uint8
FP8X4 = mybir.dt.float8_e4m3fn_x4
COPY = mybir.ActivationFunctionType.Copy
IDENTITY = mybir.ActivationFunctionType.Identity
MULT = mybir.AluOpType.mult
ADD = mybir.AluOpType.add

P = 128
LIST_ROWS = 16
KS_ROW = 32
QN_ROW = P - B
CHUNKS = N // P
NORMS = (128, 384, 512)
KN_BYTES = N * 4
PRODUCT = 256
STORES = (128, 128, 256, 256, 256)
ALIGN = 256
HEAD = 3 * POOL // 4


def tile_attend_lq_dist_topk_kernel(tc, qT, k_words, k_scales, kn, qn, offq, offs, out):
    nc = tc.nc
    with ExitStack() as ctx:
        sb = ctx.enter_context(tc.tile_pool(name="sb", bufs=1))
        shared = ctx.enter_context(tc.tile_pool(name="shared", bufs=1))
        ps = ctx.enter_context(tc.psum_pool(name="ps", bufs=1))

        offs_sb = sb.tile([P, B * N // LIST_ROWS], U16, name="offs_sb", align_bytes=ALIGN)
        offq_sb = sb.tile([P, B * NQ // LIST_ROWS], U16, name="offq_sb", align_bytes=ALIGN)
        kn_sb = sb.tile([P, T], F32, name="kn_sb", align_bytes=ALIGN)
        ks_sb = sb.tile([P, T], U8, name="ks_sb", align_bytes=ALIGN)
        kw_sb = sb.tile([P, T], I32, name="kw_sb", align_bytes=ALIGN)
        qn_rows = sb.tile([P, NQ], F32, name="qn_rows", align_bytes=ALIGN)
        ks_operand = sb.tile([P, B * N], U8, name="ks_operand", align_bytes=ALIGN)
        ident = sb.tile([P, P], F32, name="ident")
        early = sb.tile([P, 2 * POOL], F32, name="early", align_bytes=ALIGN)
        third = sb.tile([P, POOL], F32, name="third", align_bytes=ALIGN)
        last = sb.tile([P, POOL], F32, name="last", align_bytes=ALIGN)

        nc.vector.memset(ks_sb[:].bitcast(I32), 0)
        nc.vector.memset(kn_sb[0 : P - 1, :], 0.0)
        make_identity(nc, ident[:])

        q_rows = qT.rearrange("(p t) c -> p (t c)", t=4)
        nc.sync.dma_start(early[:, 0:HEAD], q_rows[:, 0:HEAD])
        nc.sync.dma_start(offs_sb[:], offs)
        nc.scalar.dma_start(kn_sb[P - 1 : P, :], kn[0:1, :])
        nc.scalar.dma_start(qn_rows[QN_ROW:P, :], qn.rearrange("b q o -> b (q o)"))
        nc.sync.dma_start(ks_sb[KS_ROW : KS_ROW + 64 : 4, :].bitcast(I32), k_scales[0].bitcast(I32))
        nc.sync.dma_start(kw_sb[:], k_words[0].rearrange("p n t -> p (n t)").bitcast(I32))
        nc.sync.dma_start(offq_sb[:], offq)
        nc.sync.dma_start(early[:, HEAD : 2 * POOL], q_rows[:, HEAD : 2 * POOL])
        nc.sync.dma_start(third[:], q_rows[:, 2 * POOL : 3 * POOL])
        nc.sync.dma_start(last[:], q_rows[:, 3 * POOL : 4 * POOL])
        nc.scalar.activation(qn_rows[0:QN_ROW, :], kn_sb[0:QN_ROW, 0:NQ], COPY)

        list_cols = NQ // LIST_ROWS
        q_lists = [offq_sb[:, b * list_cols : (b + 1) * list_cols] for b in range(B)]
        slot_cols = N // LIST_ROWS

        ks_g = sb.tile([P, B * N], U8, name="ks_g", align_bytes=ALIGN)
        nc.vector.tensor_copy(ks_g[:], ks_sb[:].indirect(offs_sb[:]))
        cut = B * N - PRODUCT
        moves = [(Q, c0, c1) for c0, c1 in ((0, cut), (cut, B * N)) for Q in range(4)]
        for Q, c0, c1 in moves:
            rows = ks_g[KS_ROW + 16 * Q : KS_ROW + 16 * Q + 16 : 4, c0:c1]
            nc.sync.dma_start(ks_operand[32 * Q : 32 * Q + 4, c0:c1].bitcast(I32), rows.bitcast(I32))
        kw_g = sb.tile([P, B * N], U32, name="kw_g", align_bytes=ALIGN)
        nc.vector.tensor_copy(kw_g[:], kw_sb[:].bitcast(U32).indirect(offs_sb[:]))

        kn_g = [shared.tile([P, N], F32, name=f"kn_g{b}", offset=b * KN_BYTES) for b in range(B)]
        for b in range(B):
            nc.scalar.activation(kn_g[b][:], kn_sb[:].indirect(offs_sb[:, b * slot_cols : (b + 1) * slot_cols]), COPY)
        qn_turned = ps.tile([P, P], F32, name="qn_turned", tag=f"bank{B}")
        nc.tensor.transpose(qn_turned[:], qn_rows[:], ident[:])
        qn_cols = sb.tile([P, B], F32, name="qn_cols")
        nc.scalar.activation(qn_cols[:], qn_turned[:, QN_ROW:P], COPY)
        cols = [sb.tile([P, CHUNKS], F32, name=f"cols{b}") for b in range(B)]
        spreads = [ps.tile([P, w], F32, name=f"spread{h}", tag=f"spread{h}") for h, w in enumerate(NORMS)]
        starts = [sum(NORMS[:h]) for h in range(len(NORMS))]

        def piece(slot):
            h = max(h for h in range(len(NORMS)) if starts[h] <= slot)
            return h, slot - starts[h]

        def spread(b, j):
            h, c0 = piece(b * N + j * P)
            nc.tensor.transpose(spreads[h][:, c0 : c0 + P], cols[b][:, j : j + 1].to_broadcast([P, P]), ident[:])

        for b in range(B):
            kn_turned = ps.tile([P, CHUNKS, P], F32, name=f"kn_turned{b}", tag="bank0")
            for j in range(CHUNKS):
                nc.tensor.transpose(kn_turned[:, j, :], kn_g[b][:, j * P : (j + 1) * P], ident[:])
            nc.scalar.activation(cols[b][:], kn_turned[:, :, P - 1], COPY)
            if b == 0:
                spread(0, 0)
        for slot in range(P, B * N, P):
            spread(slot // N, slot % N // P)

        first_norms = sb.tile([P, NORMS[0]], F32, name="first_norms", align_bytes=ALIGN)
        nc.vector.tensor_scalar_add(first_norms[:], spreads[0][:], qn_cols[:, 0:1])
        q_g = [sb.tile([P, NQ, 4], BF16, name=f"q_g{b}", align_bytes=ALIGN) for b in range(B)]
        low = [shared.tile([P, 2, NQ], F32, name=f"low{b}", offset=b * KN_BYTES // 2) for b in range(B)]
        high = shared.tile([P, 2, NQ], F32, name="high", offset=KN_BYTES)
        for b in range(B):
            for t in range(2):
                nc.scalar.activation(low[b][:, t, :], early[:, t * POOL : (t + 1) * POOL].indirect(q_lists[b]), COPY)
        nc.scalar.activation(high[:, 0, :], third[:].indirect(q_lists[1]), COPY)
        nc.scalar.activation(high[:, 1, :], last[:].indirect(q_lists[1]), COPY)
        nc.vector.tensor_copy(q_g[0][:, :, 2], third[:].indirect(q_lists[0]))
        nc.vector.tensor_copy(q_g[0][:, :, 0:2], low[0][:].rearrange("p t n -> p n t"))
        nc.vector.tensor_copy(q_g[0][:, :, 3], last[:].indirect(q_lists[0]))
        nc.vector.tensor_copy(q_g[1][:, :, 0:2], low[1][:].rearrange("p t n -> p n t"))
        later_norms = sb.tile([P, B * N - NORMS[0]], F32, name="later_norms", tag="last", align_bytes=ALIGN)
        norms = [first_norms[:], later_norms[:, 0 : NORMS[1]], later_norms[:, NORMS[1] :]]
        for h in (2, 1):
            b = starts[h] // N
            nc.scalar.activation(norms[h], spreads[h][:], IDENTITY, bias=qn_cols[:, b : b + 1])

        q_codes = [sb.tile([P, NQ], U32, name=f"q_codes{b}", align_bytes=ALIGN) for b in range(B)]
        q_scales = [sb.tile([P, NQ], U8, name=f"q_scales{b}", align_bytes=ALIGN) for b in range(B)]

        def quantise(b):
            nc.vector.quantize_mx(
                out=q_codes[b][:].bitcast(FP8X4),
                scales=q_scales[b][:],
                in_=q_g[b][:].rearrange("p n t -> p (n t)"),
            )

        quantise(0)
        nc.vector.tensor_copy(q_g[1][:, :, 2:4], high[:].rearrange("p t n -> p n t"))
        quantise(1)
        products = []
        for i in range(B * N // PRODUCT):
            slots = slice(i * PRODUCT, (i + 1) * PRODUCT)
            b = slots.start // N
            acc = ps.tile([P, PRODUCT], F32, name=f"acc{i}", tag=f"bank{i}")
            nc.tensor.matmul_mx(
                out=acc[:],
                lhsT=q_codes[b][:].bitcast(FP8X4),
                lhsT_scale=q_scales[b][:],
                rhs=kw_g[:, slots].bitcast(FP8X4),
                rhs_scale=ks_operand[:, slots],
                start=True,
                stop=True,
            )
            products.append(acc)
        slot0 = 0
        for i, width in enumerate(STORES):
            b, n0 = divmod(slot0, N)
            k, a0 = divmod(slot0, PRODUCT)
            h, c0 = piece(slot0)
            res = sb.tile([P, width], F32, name=f"res{i}", align_bytes=ALIGN)
            nc.vector.scalar_tensor_tensor(
                res[:], products[k][:, a0 : a0 + width], -2.0, norms[h][:, c0 : c0 + width], MULT, ADD
            )
            nc.sync.dma_start(out[b, :, n0 : n0 + width], res[:])
            slot0 = slot0 + width
